import numpy as np, ml_dtypes
CORES = [40,64,80,88,96,104,120,144]
N = 8
import mx_ref
BF = ml_dtypes.bfloat16
def gentries(a):
    return np.ascontiguousarray(a.reshape(8, 16, -1).transpose(0, 2, 1)).reshape(8, -1)
def gtable(e):
    e = np.asarray(e); return np.ascontiguousarray(e.reshape(8, -1, 16).transpose(0, 2, 1)).reshape(128, -1).astype(np.int32)
def gcols(t, e):
    v = np.concatenate([t.reshape(8, 16, -1, 4), np.zeros((8, 16, 1, 4), BF)], axis=2)
    return np.ascontiguousarray(np.stack([v[g][:, e[g]] for g in range(8)])).reshape(128, -1)
def tile(rs):
    return np.stack(rs, axis=2).reshape(128, -1).astype(BF)
def pick(q, e):
    c = np.concatenate([q[0].reshape(128, -1, 4), np.zeros((128, 1, 4), np.uint8)], axis=1); s = np.concatenate([q[1], np.ones((16, 1), np.uint8)], axis=1)
    return (np.ascontiguousarray(c[:, e].reshape(128, -1)), np.ascontiguousarray(s[:, e]))
def join(*qs):
    return (np.concatenate([q[0] for q in qs], axis=1), np.concatenate([q[1] for q in qs], axis=1))
def put(q, e, v):
    c, s = q[0].reshape(128, -1, 4).copy(), q[1].copy(); c[:, e] = v[0].reshape(128, -1, 4); s[:, e] = v[1]
    return (c.reshape(128, -1), s)
def pk(c, s):
    return (np.ascontiguousarray(c), mx_ref.live(s))
def emit(q):
    return q[0], q[1]
def packed(v, rng):
    q = [mx_ref.quantize(np.ascontiguousarray(v[r])) for r in range(N)]
    return np.stack([a for a, b in q]), np.stack([mx_ref.plane(b, rng) for a, b in q])
def values_of_codes():
    e, c = np.zeros((128, 128, 4), np.float32), np.zeros((128, 2, 4), np.uint8)
    e[np.arange(128), np.arange(128), 0] = 1
    c[:127, :, 0] = np.arange(256).reshape(2, 128).T[:127]
    return mx_ref.matmul(mx_ref.quantize(e.reshape(128, 512).astype(BF)), (c.reshape(128, 8), np.full((16, 2), 127, np.uint8))).T.reshape(-1).astype(np.float64)
CODE_VALUE, SCALE_VALUE = values_of_codes(), 2.0 ** (np.arange(256) - 127.0)
def decode(q):
    return (CODE_VALUE[q[0]].reshape(16, 8, -1, 4) * SCALE_VALUE[q[1]][:, None, :, None] + 0.0).reshape(128, -1).astype(np.float32)
def f(rng, *shape):
    return mx_ref.flush((rng.standard_normal(shape, dtype=np.float32) * np.exp2(rng.integers(-2, 3, shape[:-1] + (1,)))).astype(BF))
def wide(rng, *shape, cols=0):
    v = rng.standard_normal(shape, dtype=np.float32) * np.exp2(rng.integers(-12, 13, shape)).astype(np.float32)
    if cols: v *= np.repeat(np.exp2(rng.integers(-cols, cols + 1, shape[:-2] + (1, shape[-1] // 4))) * (rng.random(shape[:-2] + (1, shape[-1] // 4)) > 0.0625), 4, axis=-1).astype(np.float32)
    return mx_ref.flush(v.astype(BF))
C, HALF = 352, 176
STEP = [1, 2, 4]
def numbers_of(rng):
    return {"x": np.array(f(rng, N, 128, 4 * C)), "lv": np.array(f(rng, N, 128, 4 * C)), "u": np.array(f(rng, N, 128, 512)), "v": np.array(f(rng, N, 128, 512))}
def names(rng):
    return rng.permuted(np.tile(np.arange(2 * C), (N, 8, 1)), axis=2)
def paired(rng, roots):
    p, n = np.flatnonzero(roots), np.flatnonzero(~roots)
    k = np.zeros(2 * C, np.int64)
    k[p] = rng.permutation(n)
    k[np.concatenate([n, np.arange(C, 2 * C)])] = rng.permutation(np.concatenate([p, np.arange(C, 2 * C)]))
    return k
def stored(k):
    return {"lt": np.stack([gtable(k[r][:, :C]) for r in range(N)]), "rt": np.stack([gtable(k[r][:, C:]) for r in range(N)])}
def layers(rng):
    return np.array(f(rng, N, 128, 2048)).reshape(N, 8, 16, 4, 8, 16, 4)
def weights(rng, w):
    c, p = packed(np.ascontiguousarray(w).reshape(N, 128, 2048), rng)
    return {"wc": c, "ws": p}
def setup_inputs(rng):
    return {**numbers_of(rng), **stored(names(rng)), **weights(rng, layers(rng))}
def setup_inputs_ties(rng):
    d = numbers_of(rng)
    o = rng.permutation(N)
    k = rng.integers(-1, 2, (N, 8, 4, C)).astype(np.float32)
    k[o[1]] = 1
    e = names(rng)
    for g in range(8):
        p = rng.permutation(C) < HALF
        k[o[3], g, 0] = np.where(p, 1.0, -1.0)
        if g % 2:
            k[o[3], g, 1] = np.minimum(k[o[3], g, 1], 0)
            k[o[3], g, 2] = k[o[3], g, 0]
        e[o[3], g] = paired(rng, p)
    x = d["x"].reshape(N, 8, 16, C, 4)
    x[:, :, :8] = 0
    x[:, :, :4, :, 0] = k.astype(BF)
    c = np.ones(N, np.float32)
    c[o[0]] = 0
    c[o[2]] = -1
    u = d["u"].reshape(N, 128, 128, 4)
    for g in range(8):
        for h in range(16 * g, 16 * g + 4):
            u[:, :, h] = 0
            u[:, h, h, 0] = c.astype(BF)
    w = layers(rng)
    w[:, :, :, :, :, :8] = 0
    return {"x": x.reshape(N, 128, 4 * C), "lv": d["lv"], "u": u.reshape(N, 128, 512), "v": d["v"], **stored(e), **weights(rng, w)}
def setup_inputs_near(rng):
    d = numbers_of(rng)
    o = rng.permutation(N)
    t = int(np.flatnonzero(o == 0)[0])
    k = np.where(o % 2 == 0, 2.0 ** -30, 1.0).astype(np.float32)
    x = d["x"].astype(np.float32).reshape(N, 8, 16, C, 4)
    lv = d["lv"].astype(np.float32).reshape(N, 8, 16, C, 4)
    s = rng.integers(-1, 2, (N, 8, 4, C)) * np.where(o % 2 == 0, 2.0 ** -28, 1.0)[:, None, None, None]
    x[:, :, :8] = 0
    x[:, :, :4, :, 0] = 1.125 * s
    x[:, :, 4:8, :, 0] = -1.25 * s
    for r in range(N):
        at = [0, C - 1, int(rng.integers(C)), int(rng.integers(C))]
        for g, j in zip(rng.permutation(8)[:4], at): x[r, g, rng.integers(4), j, 0] = 2.0 ** 30 * rng.choice([-1.0, 1.0])
    x[t] = 0
    x[t, :, 7, :, 3] = 2.0 ** -29
    for z in (x, lv):
        z[:, :, 15, :, 3] = 4.0
        z[t, :, 8:] = rng.choice([-1.0, 1.0], (8, 8, C, 4)) * 2.0 ** -26
        z[t, :, 8:12, :, 0] *= np.float32(2.0 ** -4)
        z[t, ::2, 9:12:2, :, 0] = 2.0 ** -30
        z[t, :, 15, :, 3] = 2.0 ** -28
    u = d["u"].reshape(N, 128, 128, 4)
    w = layers(rng)
    w[:, :, :8] = 0
    w[:, :, :, :, :, :8] = 0
    w[:, :, :, 3, :, 15] = 0
    w[:, :, 15, 3, :, 15, 3] = 4.0
    w[t, :, 15, 3, :, 7, 3] = 4.0
    for g in range(8):
        for i in range(4):
            h = 16 * g + i
            u[:, :, h] = 0
            u[:, h, h, 0] = (1.125 * k).astype(BF)
            u[:, h + 4, h, 0] = k.astype(BF)
            u[t, :, h] = 0
            u[t, h, h, 1] = 1.125 * 2.0 ** -30
            u[t, h + 4, h, 1] = 2.0 ** -30
            w[t, g, 8 + i, 1, g, i, 0] = 1.125 * 2.0 ** -5
            w[t, g, 8 + i, 1, g, i + 4, 0] = -1.25 * 2.0 ** -5
    return {"x": x.reshape(N, 128, 4 * C).astype(BF), "lv": lv.reshape(N, 128, 4 * C).astype(BF), "u": u.reshape(N, 128, 512), "v": d["v"], **stored(names(rng)), **weights(rng, w)}
def setup_inputs_odd(rng):
    d = numbers_of(rng)
    x = np.zeros((N, 8, 16, C, 4), np.float32)
    lv = np.zeros((N, 8, 16, C, 4), np.float32)
    a = np.exp2(rng.integers(5, 9, (8, 1)).astype(np.float32))
    b = rng.integers(0, 2, (N, 8, 4, C))
    x[:, :, 0, :, 3] = 1.96875 * 2.0 ** 8
    x[:, :, 0:8:2, :, 0] = (8 + b) * 2.0 ** -8
    x[:, :, 1:8:2, :, 0] = (9 - b) * 2.0 ** -8
    for t in (x, lv):
        t[:, :, 7, :, 1] = 1.125 * a
        t[:, :, 7, :, 2] = 0.0703125 * a
    x[:, :, 9, :, 0] = -a
    u = d["u"].reshape(N, 128, 128, 4)
    w = np.zeros((N, 8, 16, 4, 8, 16, 4), np.float32)
    for g in range(8):
        w[:, g, 7, 0, g, 9, 1] = 28.0
        for i in range(4):
            u[:, :, 16 * g + i] = 0
            u[:, 16 * g + 2 * i, 16 * g + i, 0] = 1.0
            u[:, 16 * g + 2 * i + 1, 16 * g + i, 0] = -1.0
            w[:, g, 7, i, g, 10, 2] = [1.0, 1.25, 0.75, 0.5625][i] * 2.0 ** -5
    return {"x": x.reshape(N, 128, 4 * C).astype(BF), "lv": lv.reshape(N, 128, 4 * C).astype(BF), "u": u.reshape(N, 128, 512), "v": d["v"], **stored(names(rng)), **weights(rng, w.astype(BF))}
def setup_inputs_ends(rng):
    d = numbers_of(rng)
    n = np.arange(N)
    o = np.array([1, 0, 2, 3])[(n & 3) ^ rng.integers(0, 4, 2)[n >> 2]]
    x = np.zeros((N, 8, 16, C, 4), np.float32)
    lv = np.zeros((N, 8, 16, C, 4), np.float32)
    a = np.zeros((N, 8, 4))
    k = names(rng)
    w = np.zeros((N, 128, 4, 128, 4), np.float32)
    i, c = np.arange(128), np.arange(C)
    for r in range(N):
        a[r] = rng.choice([-1.0, 1.0], (8, 4)) * (rng.permutation(8) > 1)[:, None]
        roots = rng.permutation(C) < HALF
        s = rng.choice([-1.0, 1.0], (2, 8, 16, C, 4))
        size = (0.6 + 0.05 * rng.random((2, 8, 16, C, 4))) * 2.0 ** 30
        if o[r] == 0:
            s[:] = -1.0
            k[r] = np.concatenate([2 * C - 1 - c, C - 1 - c])
        if o[r] == 1:
            s[0] = np.where(roots, 1.0, -1.0)[None, None, :, None]
            for g in range(8): k[r, g] = paired(rng, ~roots if a[r, g, 0] < 0 else roots)
        if o[r] == 2: k[r] = np.concatenate([(c + 1) % C, 2 * C - 1 - c])
        if o[r] == 3:
            s[0] = s[0][:, :1, :, :1]
            size[:] = 2.0 ** -28
            for j, g in enumerate(rng.permutation(8)):
                k[r, g] = np.concatenate([rng.permutation(C) + C * (j % 2), rng.permutation(C) + C * (1 - j % 2)])
        x[r], lv[r] = s * size
        if o[r] == 2: w[r] = rng.choice([-1.0, 1.0], (128, 4, 128, 4)) * 2.0 ** -6
        else:
            for b in range(4): w[r, i, b, i, b] = -1.0 if o[r] < 2 else 64.0
    size = np.where(o == 3, 2.0 ** -30, 2.0 ** 30)
    u = d["u"].reshape(N, 128, 128, 4)
    for j in range(4): u[:, :, j::16] = (a[:, :, j] * size[:, None] + 0.0).astype(np.float32).astype(BF)[:, None, :, None]
    v = rng.choice([-1.0, 1.0], (N, 128, 512)) * size[:, None, None]
    return {"x": x.reshape(N, 128, 4 * C).astype(BF), "lv": lv.reshape(N, 128, 4 * C).astype(BF), "u": u.reshape(N, 128, 512), "v": v.astype(np.float32).astype(BF), **stored(k), **weights(rng, w.astype(BF))}
def setup_inputs_spread(rng):
    d = setup_inputs(rng)
    d["x"] = wide(rng, N, 128, 4 * C, cols=6)
    d["lv"] = wide(rng, N, 128, 4 * C, cols=6)
    return d
def check_inputs(d):
    b = []
    for k in ("x", "lv", "u", "v"):
        a = np.abs(d[k].astype(np.float32))
        if not (np.isfinite(a).all() and ((a == 0) | (a >= 2.0 ** -30) & (a <= 2.0 ** 30)).all()): b.append("a value of " + k)
    none, least, most = [emit(mx_ref.quantize(np.full((128, 16), k, np.float32).astype(BF)))[1][0, 0] for k in (0.0, 2.0 ** -6, 2.0 ** 6)]
    for r in range(N):
        if (np.sort(np.concatenate([gentries(d["lt"][r]), gentries(d["rt"][r])], axis=1), axis=1) != np.arange(2 * C)).any(): b.append("lt and rt: not every name once in a group")
        if ((d["wc"][r] == 0x7F) | (d["wc"][r] == 0xFF)).any(): b.append("wc: a code that is no number")
        s = mx_ref.live(d["ws"][r])
        if ((s != none) & ((s < least) | (s > most))).any(): b.append("ws: a scale out of range")
        if (((d["wc"][r].reshape(16, 8, 512, 4) & 0x7F) != 0) & (s == none)[:, None, :, None]).any(): b.append("wc: a code other than zero under the scale of zeros")
    return b
def rewrite(left, right, act, turn):
    g, c = np.nonzero((left < C) & (act > 0) & (np.take_along_axis(act, left % C, 1) < 0))
    s = left[g, c]
    a, b, z = left[g, s], right[g, s], right[g, c]
    t = turn[g, a % C] > 0
    left, right = left.copy(), right.copy()
    left[g, c], right[g, c] = np.where(t, a, s), np.where(t, s, b)
    left[g, s], right[g, s] = np.where(t, b, a), z
    return left, right
def reference(x, lv, u, v, lt, rt, wc, ws):
    qu = [mx_ref.quantize(u[r]) for r in range(N)]
    lay = [pk(wc[r], ws[r]) for r in range(N)]
    left, right = [gentries(lt[r]) for r in range(N)], [gentries(rt[r]) for r in range(N)]
    now, leaf = [x[r] for r in range(N)], [lv[r] for r in range(N)]
    for step in STEP:
        made = []
        for r in range(N):
            s = mx_ref.matmul(qu[r], mx_ref.quantize(now[r])).reshape(8, 16, C)
            for j in range(2): left[r], right[r] = rewrite(left[r], right[r], s[:, 2 * j], s[:, 2 * j + 1])
            win = np.concatenate([now[r], leaf[r]], axis=1)
            z = mx_ref.quantize(((gcols(win, left[r]).astype(np.float32) + gcols(win, right[r]).astype(np.float32)) * np.float32(0.5)).astype(BF))
            made.append(tile([mx_ref.matmul(pick(lay[r], np.arange(128 * b, 128 * b + 128)), z) * np.float32(0.03125) for b in range(4)]))
        for r in range(N):
            p = r ^ step
            m = np.take_along_axis(left[p], right[r] % C, 1) % C
            far = gcols(decode(mx_ref.quantize(made[p])).astype(BF), m[:, :HALF])
            leaf[r] = np.concatenate([far, gcols(made[r], m[:, HALF:])], axis=1)
            now[r] = (now[r].astype(np.float32) + leaf[r].astype(np.float32)).astype(BF)
    y, gr = np.zeros((N, 128, C), np.float32), np.zeros((N, 8, 2 * C), np.float32)
    oc, osc = np.zeros((N, 128, 4 * C), np.uint8), np.zeros((N, 16, C), np.uint8)
    for r in range(N):
        q = mx_ref.quantize(now[r])
        y[r] = mx_ref.matmul(mx_ref.quantize(v[r]), q)
        gr[r] = np.concatenate([left[r], right[r]], axis=1)
        oc[r], osc[r] = emit(q)
    return {"y": y, "gr": gr, "oc": oc, "osc": osc}

@@ -1,0 +1,577 @@
+from concourse.bass import DstId, RemoteDMATransfer
+from concourse.mybir import dt, AluOpType, ActivationFunctionType
+
+Op, Act = AluOpType, ActivationFunctionType
+C, HALF, K = 352, 176, 22
+STEP = [1, 2, 4]
+FR, F10 = 2.0 ** -22, 2.0 ** 10
+CHUNKS = [(0, 192), (192, 352)]
+WIDE = [("LR0", 44), ("LR1", 44), ("CB", 44), ("F", 66), ("LH", 44), ("D", 44), ("E", 44), ("Q", 44), ("SS", 44), ("M1", 44), ("M2", 44), ("M3", 44),
+        ("N1", 44), ("N2", 44), ("N3", 44), ("N4", 44), ("t1", 44), ("t2", 44), ("par", 22), ("x", 22), ("i32", 22), ("A", 22), ("dlp", 22), ("aM", 22),
+        ("o", 22), ("I", 22), ("vA", 22), ("vN", 22), ("mi", 22), ("mt", 22), ("mm", 22), ("c704", 22)]
+U16S = [("OLs", 44), ("OL1", 22), ("OLC0", 22), ("OLC1", 22), ("O", 22), ("SL0", 44), ("SL1", 44), ("LX", 22), ("MO", 22)]
+FTHS = [("tA", 22), ("tP", 22), ("tN", 22), ("tQ", 22), ("pk", 22), ("px", 8)]
+
+
+def places(blocks):
+    at, d = 0, {}
+    for n, w in blocks:
+        d[n] = at
+        at += (w + 7) // 8 * 8
+    return d, at
+
+
+WI, WIN_ = places(WIDE)
+WU, WUN = places(U16S)
+WF, WFN = places(FTHS)
+
+
+def codes_of(name, n):
+    return {"q" + name: ("sbuf", [128, n], "float8_e4m3fn_x4"), "s" + name: ("sbuf", [128, n], "uint8")}
+
+
+def tiles(kind, **widths):
+    return {k: ("sbuf", [128, w], kind) for k, w in widths.items()}
+
+
+SCRATCH = {
+    **tiles("bfloat16", xt=4 * C, lvt=4 * C, ut=512, vt=512, win=8 * C, gl=4 * C, zt=4 * C, hp=4 * C, gt=4 * HALF, et=2048, one=512, kmb=C, e1b=C, e2b=C, e1s=C, e2s=C, twb=C, dmb=C),
+    **codes_of("x", C), **codes_of("u", 128), **codes_of("ur", 512), **codes_of("v", 128), **codes_of("w", 512), **codes_of("e", 512), **codes_of("z", C),
+    **tiles("int32", lw=K, rw=K, wi=WIN_, ui=32),
+    **tiles("uint16", wu=WUN, ux=32),
+    **tiles("float32", wf=WFN, ones=32, ex=704, tr=704, kr=C, dm=C, km=C, rc=C, none=C, wa=4 * C, wb=4 * C, lrf=C, lrs=C, a1=C, tw0=2 * C, tw1=4 * C,
+            pw0=2 * C, sg0=C, sg1=C, sgt=C, pf0=C, pf1=2 * C, e1=C, e2=C, gg=C, e3=C, gro=2 * C, yo=C, ll=2 * C),
+}
+for _b in range(8):
+    SCRATCH["ps%d" % _b] = ("psum", [128, 512], "float32")
+for _r in range(3):
+    for _n in ("so", "ro", "la"):
+        SCRATCH["%sR%d" % (_n, _r)] = ("sbuf", [128, 2 * K if _n == "so" else K], "uint16")
+        SCRATCH["%sM%d" % (_n, _r)] = ("sbuf", [128, 11], "uint16")
+        SCRATCH["%sQ%d" % (_n, _r)] = ("sbuf", [128, HALF], "float8_e4m3fn_x4")
+        SCRATCH["%sS%d" % (_n, _r)] = ("sbuf", [128, HALF], "uint8")
+LOADS = ["lt", "rt", "x", "u", "lv", "wc", "ws", "v"]
+SEMAPHORES = (["cv", "cs", "ct", "cp", "ls", "outs"] + ["ld_" + n for n in LOADS]
+              + ["a%s%d" % (n, r) for n in "RMCS" for r in range(3)])
+
+
+def route(topo, core, partner):
+    ok = [c for c in topo.cores_of(core) if c != core and topo.may_write(c, partner)]
+    near = [c for c in ok if topo.die(c) == topo.die(core)]
+    far = [c for c in ok if topo.die(c) != topo.die(core)]
+    return near[0], far[0], near[1]
+
+
+def bits(engines):
+    return sum(1 << e for e in engines)
+
+
+def sent_on(kind, rd):
+    return 16 if kind == "S" or (kind == "R" and rd) else 8
+
+
+def relay_program(g, core, T, topo, rank):
+    src, sent = T.cores[rank], 0
+    for rd, s in enumerate(STEP):
+        dst = T.cores[rank ^ s]
+        a, b, c = route(topo, src, dst)
+        if core not in (a, b, c):
+            continue
+        rid, pid = topo.addr(dst, core)
+        eng = topo.engines(core, dst)[:8]
+        jobs = {a: [("R", "R", 0, K), ("C", "Q", 0, 88)], b: [("C", "Q", 88, HALF)], c: [("M", "M", 0, 11), ("S", "S", 0, HALF)]}[core]
+        for sem, buf, lo, hi in jobs:
+            g.wait_ge(T.sem["a%s%d" % (sem, rd)], sent_on(sem, rd))
+            o, i = T["la%s%d" % (buf, rd)][:, lo:hi], T["ro%s%d" % (buf, rd)][:, lo:hi]
+            if buf == "Q":
+                o, i = o.bitcast(dt.uint8), i.bitcast(dt.uint8)
+            g.remote_dma(o, i, T.sem["a%s%d" % (sem, rd)], T.sem["ls"], pid, rid, bits(eng))
+            sent += len(eng)
+    if sent:
+        g.wait_ge(T.sem["ls"], sent)
+
+
+def rank_program(g, core, T, topo):
+    rank = T.rank_of(core)
+    if rank is None:
+        for c in topo.cores_of(core):
+            if T.rank_of(c) is not None:
+                relay_program(g, core, T, topo, T.rank_of(c))
+        return
+
+    eng = {"v": g.vector, "s": g.scalar, "t": g.tensor, "p": g, "y": g.sync}
+    done = {"v": "cv", "s": "cs", "t": "ct", "p": "cp"}
+    count = {"cv": 0, "cs": 0, "ct": 0, "cp": 0, "outs": 0, "ls": 0}
+    known = {q: {} for q in eng}
+    uses = {}
+    clocks = {}
+
+    def meet(a, b):
+        if a[1] >= b[2] or b[1] >= a[2]:
+            return False
+        return not (a[3] == b[3] and a[3] > 1 and (a[1] - b[1]) % a[3])
+
+    def before(q, reads, writes):
+        need = {}
+        for w, regs in ((False, reads), (True, writes)):
+            for r in regs:
+                ps = r[0][:2] == "ps"
+                for (o, ow, oq, tok) in uses.get(r[0], []):
+                    if (w or ow or (ps and oq != q)) and meet(r, o):
+                        need[tok[0]] = max(need.get(tok[0], 0), tok[1])
+        k = known[q]
+        for s in sorted(need, key=lambda s: s in ("cv", "cs", "ct", "cp")):
+            if k.get(s, 0) < need[s]:
+                eng[q].wait_ge(T.sem[s], need[s])
+                k[s] = need[s]
+                for a, b in clocks.get((s, need[s]), {}).items():
+                    k[a] = max(k.get(a, 0), b)
+
+    def note(q, tok, reads, writes):
+        clocks[tok] = dict(known[q])
+        for r in writes:
+            uses[r[0]] = [u for u in uses.get(r[0], []) if not (r[3] in (1, u[0][3]) and r[1] <= u[0][1] and u[0][2] <= r[2] and (u[0][1] - r[1]) % r[3] == 0)]
+        for w, regs in ((False, reads), (True, writes)):
+            for r in regs:
+                uses.setdefault(r[0], []).append((r, w, q, tok))
+
+    def run(q, fn, reads, writes):
+        before(q, reads, writes)
+        s = done[q]
+        count[s] += 1
+        fn().then_inc(T.sem[s], 1)
+        note(q, (s, count[s]), reads, writes)
+
+    def load(q, sem, out, in_, reg):
+        before(q, [], [reg])
+        eng[q].dma_start(out, in_).then_inc(T.sem[sem], 16)
+        note(q, (sem, 16), [], [reg])
+
+    def store(q, out, in_, reg):
+        before(q, [reg], [])
+        eng[q].dma_start(out, in_).then_inc(T.sem["outs"], 16)
+        count["outs"] += 16
+
+    def R(name, lo=0, hi=None, step=1):
+        return (name, lo, SCRATCH[name][1][1] if hi is None else hi, step)
+
+    def W(name, lo=0, hi=K):
+        return ("wi", WI[name] + lo, WI[name] + hi, 1)
+
+    def U(name, lo=0, hi=K):
+        return ("wu", WU[name] + lo, WU[name] + hi, 1)
+
+    def Fl(name, lo=0, hi=K):
+        return ("wf", WF[name] + lo, WF[name] + hi, 1)
+
+    def ap(r):
+        return T[r[0]][:, r[1]:r[2]] if r[3] == 1 else T[r[0]][:, r[1]:r[2]:r[3]]
+
+    def src(r, ind):
+        return ap(r) if ind is None else ap(r).indirect(ap(ind))
+
+    def given(*rs):
+        return [r for r in rs if r is not None]
+
+    def tt(out, in0, in1, op, ind=None):
+        run("v", lambda: g.vector.tensor_tensor(ap(out), src(in0, ind), ap(in1), op), given(in0, in1, ind), [out])
+
+    def ts(out, in0, s1, op0, s2=None, op1=None):
+        if op1 is None:
+            run("v", lambda: g.vector.tensor_scalar(ap(out), ap(in0), s1, None, op0), [in0], [out])
+        else:
+            run("v", lambda: g.vector.tensor_scalar(ap(out), ap(in0), s1, s2, op0, op1), [in0], [out])
+
+    def cp(out, in_, ind=None):
+        run("v", lambda: g.vector.tensor_copy(ap(out), src(in_, ind)), given(in_, ind), [out])
+
+    def put(out, ind, in_):
+        run("v", lambda: g.vector.tensor_copy(ap(out).indirect(ap(ind)), ap(in_)), [in_, ind], [out])
+
+    def fill(out, c):
+        run("v", lambda: g.vector.memset(ap(out), c), [], [out])
+
+    def act(out, in_, ind=None, func=Act.Copy, scale=1.0):
+        if scale == 1.0:
+            run("s", lambda: g.scalar.activation(ap(out), src(in_, ind), func), given(in_, ind), [out])
+        else:
+            run("s", lambda: g.scalar.activation(ap(out), src(in_, ind), func, scale=scale), given(in_, ind), [out])
+
+    def shift(out, in_, scale, bias):
+        run("s", lambda: g.scalar.activation(ap(out), ap(in_), Act.Identity, bias=bias, scale=scale), [in_], [out])
+
+    def scan(out, d0, d1, op0, op1):
+        run("v", lambda: g.vector.tensor_tensor_scan(ap(out), ap(d0), ap(d1), 0.0, op0, op1), [d0, d1], [out])
+
+    def quant(name, tile, lo, hi, q=None, s=None):
+        q, s = q or "q" + name, s or "s" + name
+        t = R(tile, 4 * lo, 4 * hi)
+        run("v", lambda: g.vector.quantize_mx(T[q][:, lo:hi], T[s][:, lo:hi], ap(t)), [t], [R(q, lo, hi), R(s, lo, hi)])
+
+    def mm(bank, w, wlo, q, s, lo, hi):
+        p, wq, wsc = "ps%d" % bank, "q" + w, "s" + w
+        run("t", lambda: g.tensor.matmul_mx(T[p][:, 0:hi - lo], T[wq][:, wlo:wlo + 128], T[wsc][:, wlo:wlo + 128], T[q][:, lo:hi], T[s][:, lo:hi], True, True),
+            [R(wq, wlo, wlo + 128), R(wsc, wlo, wlo + 128), R(q, lo, hi), R(s, lo, hi)], [R(p)])
+
+    def arrive(name, sem, n):
+        note("p", (sem, n), [], [R(name)])
+        clocks[(sem, n)] = {}
+
+    def send(rds, fn, n):
+        before("p", rds, [])
+        fn()
+        count["ls"] += n
+
+    def masked(out, row):
+        scan(out, row, R("dm"), Op.add, Op.mult)
+
+    def pick(out, row):
+        scan(out, R("km"), row, Op.mult, Op.add)
+
+    def ends(name):
+        return (name, 15, C, 16)
+
+    def col16(out, x):
+        w = x[2] - x[1]
+        ts(W("t1", 0, w), x, float(C), Op.is_ge, -float(C), Op.mult)
+        tt(W("t2", 0, w), x, W("t1", 0, w), Op.add)
+        cp(out, W("t2", 0, w))
+
+    def iota(out, pattern, base, cm):
+        if out[0] in ("kr", "rc"):
+            run("p", lambda: g.iota(ap(out), pattern, base, cm, allow_small_or_imprecise_dtypes=True), [], [out])
+        else:
+            run("p", lambda: g.iota(ap(out), pattern, base, cm), [], [out])
+
+    load("y", "ld_lt", T["lw"][:], T["lt"][:], R("lw"))
+    load("s", "ld_rt", T["rw"][:], T["rt"][:], R("rw"))
+    load("y", "ld_u", T["ut"][:], T["u"][:], R("ut"))
+    load("s", "ld_x", T["xt"][:], T["x"][:], R("xt"))
+    load("y", "ld_lv", T["lvt"][:], T["lv"][:], R("lvt"))
+    load("y", "ld_wc", T["qw"][:, 0:512].bitcast(dt.uint8), T["wc"][:, 0:2048], R("qw"))
+    load("y", "ld_ws", T["sw"][:, 0:512], T["ws"][:, 0:512], R("sw"))
+    load("y", "ld_v", T["vt"][:], T["v"][:], R("vt"))
+
+    iota(W("x"), [[0, K]], 0, 1)
+    iota(R("kr"), [[0, K], [1, 16]], 0, 0)
+    iota(W("i32"), [[32, K]], 0, 0)
+    iota(W("mm"), [[16, K]], 0, 0)
+    iota(R("ui"), [[1, 4], [16, 8]], 0, 0)
+    iota(R("rc"), [[1, C]], 0, 0)
+    fill(R("none"), float(C))
+    fill(R("ones"), 1.0)
+    fill(R("km"), 1.0)
+    fill(W("SS"), C)
+    ts(W("t1"), W("x"), 31, Op.bitwise_and)
+    ts(W("t2"), W("x"), 15, Op.bitwise_and)
+    fill(R("km", 0, C, 16), 0.0)
+    act(R("pw0", 0, C), R("none"))
+    act(R("tw0", C, 2 * C), R("none"), scale=0.0)
+    act(R("tw1", C, 2 * C), R("none"), scale=0.0)
+    act(R("kmb"), R("km"))
+    act(R("wb", 2 * C, 3 * C), R("none"), scale=0.0)
+    cp(Fl("px", 0, 8), W("t2", 0, 8))
+    tt(W("mt"), W("t1"), W("i32"), Op.add)
+    px = Fl("px", 0, 1)
+    shift(R("one", 0, C), R("none"), 0.0, 1.0)
+    shift(R("one", C, 512), R("none", 0, 160), 0.0, 1.0)
+    run("v", lambda: g.vector.tensor_scalar(T["dm"][:], T["kr"][:], ap(px), None, Op.is_equal), [R("kr"), px], [R("dm")])
+    act(R("dmb"), R("dm"))
+    cp(U("LX"), W("mt"))
+    tt(W("CB"), W("t2"), W("mm"), Op.add)
+    cp(R("ux"), R("ui"))
+    ts(W("CB", K, 2 * K), W("CB"), float(C), Op.add)
+    ts(W("c704"), W("CB"), 2.0 * C, Op.add)
+
+    ts(W("mi"), R("rw"), 1024.0, Op.mult)
+    cp(U("OLs"), R("lw"))
+    tt(Fl("pk"), W("mi"), R("lw"), Op.add)
+    for q in range(K):
+        o, i = R("ex", 32 * q, 32 * q + 32), Fl("pk", q, q + 1)
+        run("s", lambda: g.scalar.activation(ap(o), T["ones"][:], Act.Copy, scale=ap(i)), [R("ones"), i], [o])
+
+    def replicas(k):
+        a, e = 128 * k, 8 * k
+        run("v", lambda: g.vector.tensor_copy(T["qur"][:, a:a + 256].bitcast(dt.uint32), T["qu"][:, 0:128].bitcast(dt.uint32).indirect(T["ux"][:, e:e + 16])),
+            [R("qu"), R("ux")], [R("qur", a, a + 256)])
+        run("s", lambda: g.scalar.activation(T["sur"][:, a:a + 256], T["su"][:, 0:128].indirect(T["ux"][:, e:e + 16]), Act.Copy),
+            [R("su"), R("ux")], [R("sur", a, a + 256)])
+
+    def parents(pw, ol, *between):
+        f = list(between) + [lambda: None] * 2
+        put(R(pw), ol, R("rc"))
+        f[0]()
+        masked(R("e1"), R(pw, 0, C))
+        f[1]()
+        pick(R("e2"), R("e1"))
+        cp(W("par"), ends("e2"))
+
+    def start():
+        quant("u", "ut", 0, 128)
+        replicas(0)
+
+    lists = [U("OLs"), None]
+    parents("pw0", lists[0], start)
+    quant("x", "xt", 0, C)
+    run("v", lambda: g.vector.transpose(T["tr"][:], T["ex"][:]), [R("ex")], [R("tr")])
+    act(R("lrf"), R("tr"), U("LX"), scale=FR)
+    cp(W("LR0"), R("lw"))
+    cp(W("LR0", K, 2 * K), R("rw"))
+    col16(U("OLC0"), W("LR0"))
+    tt(W("dlp"), W("LR0"), W("par"), Op.subtract)
+    for b in range(4):
+        run("p", lambda: g.affine_select(T["et"][:, 512 * b:512 * b + 512], T["one"][:], [[-1, 512]], Op.is_equal, 0.0, b, 4),
+            [R("one")], [R("et", 512 * b, 512 * b + 512)])
+
+    def windows():
+        for t in range(4):
+            act(R("win", 704 * t, 704 * t + C), R("xt", t, 4 * C, 4), scale=0.5)
+
+    def scores(lo, hi, bank):
+        for k in range(2):
+            mm(bank + k, "ur", 128 * k, "qx", "sx", lo, hi)
+        act(R("sg0", lo, hi), R("ps%d" % bank, 0, hi - lo), func=Act.Sign, scale=-1.0)
+
+    def signs(lo, hi, bank):
+        ts(R("pf0", lo, hi), R("ps%d" % (bank + 1), 0, hi - lo), 0.0, Op.is_gt, 0.5, Op.mult)
+        scan(R("e1s", lo, hi), R("ps%d" % bank, 0, hi - lo), R("dm", lo, hi), Op.add, Op.mult)
+        tt(R("lrs", lo, hi), R("lrf", lo, hi), R("sg0", lo, hi), Op.add)
+        scan(R("e2s", lo, hi), R("kmb", lo, hi), R("e1s", lo, hi), Op.mult, Op.add)
+        ts(W("A", lo // 16, hi // 16), ("e2s", lo + 15, hi, 16), 0.0, Op.is_gt)
+
+    def step(rd, j, more=None, rest=None):
+        lr, ln = W("LR%d" % j, 0, 44), W("LR%d" % (1 - j), 0, 44)
+        l, r = W("LR%d" % j), W("LR%d" % j, K, 2 * K)
+        tw, pf = "tw%d" % j, R("pf%d" % j)
+        sl, sr = U("SL0", 0, K), U("SL0", K, 2 * K)
+        if j == 0:
+            tt(R(tw, 0, C), pf, R("lrs"), Op.add, U("OLC0"))
+            act(R("twb"), R(tw, 0, C))
+            more()
+        else:
+            tt(R(tw, 0, C), pf, R("lrs"), Op.add, U("OL1"))
+            act(R("twb"), R(tw, 0, C))
+            act(R("wb", 0, C), R("wa", 0, 2 * C), sl)
+            act(R("wb", C, 2 * C), R("wa", 0, 2 * C), sr)
+        own = ends("e2b")
+
+        def ownmask():
+            scan(R("e1b"), R("twb"), R("dmb"), Op.add, Op.mult)
+
+        def picked():
+            scan(R("e2b"), R("kmb"), R("e1b"), Op.mult, Op.add)
+
+        if j == 1:
+            put(R(tw, 2 * C, 4 * C), U("OL1"), R("a1"))
+            shift(R("wb", 3 * C, 4 * C), R(tw, 2 * C, 3 * C), 1.0 / F10, 1.0 / F10)
+            ownmask()
+            tt(W("dlp"), l, W("c704"), Op.subtract)
+            picked()
+            tt(W("E"), r, l, Op.subtract)
+            ts(W("A"), own, 0.0, Op.is_lt)
+            tt(W("Q"), l, W("CB"), Op.subtract)
+        tt(W("aM"), W("A"), W("dlp"), Op.mult)
+        if j == 0:
+            tt(W("E"), r, l, Op.subtract)
+        tt(W("o"), W("aM"), W("par") if j == 0 else W("c704"), Op.add)
+        if j == 0:
+            tt(W("Q"), l, W("CB"), Op.subtract)
+        cp(U("O"), W("o"))
+        tt(R("gg"), R(tw, 0, (2 if j == 0 else 3) * C), R("dm"), Op.mult, U("O"))
+        tt(W("Q", K, 2 * K), W("o"), W("CB"), Op.subtract)
+        oth = ends("e3")
+        if j == 0:
+            ownmask()
+            pick(R("e3"), R("gg"))
+            picked()
+            ts(W("I"), oth, 1.0, Op.add, 2.0 ** 22, Op.mult)
+        ts(Fl("tP"), own, 0.0, Op.is_ge, 1.5, Op.add)
+        ts(Fl("tA"), own, 0.0, Op.is_ge, 1.0, Op.add)
+        ts(Fl("tN"), own, 1.0, Op.is_ge, -1.0, Op.add)
+        ts(Fl("tQ"), own, 1.5, Op.is_ge, -1.0, Op.add)
+        if j == 0:
+            if rd == 0:
+                tt(R("wa", 0, C), R("lrf"), R("wa", 3 * C, 4 * C), Op.subtract)
+                act(R("wa", 2 * C, 3 * C), R("wa", 0, C), scale=F10)
+            rest()
+        else:
+            pick(R("e3"), R("gg"))
+        ts(W("SS", K, 2 * K), W("Q", K, 2 * K), -1.0, Op.mult, -float(C), Op.add)
+        if j == 1:
+            ts(W("I"), oth, 1.0, Op.add, 2.0 ** 22, Op.mult)
+        tt(W("vA"), oth, Fl("tA"), Op.is_ge)
+        tt(W("vN"), oth, Fl("tN"), Op.is_lt)
+        ts(W("LH"), W("I"), 1023, Op.bitwise_and)
+        ts(W("LH", K, 2 * K), W("I"), 10, Op.arith_shift_right, 1023, Op.bitwise_and)
+        tt(W("F", K, 2 * K), oth, Fl("tP"), Op.is_ge)
+        tt(W("F"), oth, Fl("tQ"), Op.is_lt)
+        tt(W("F", 2 * K, 3 * K), W("vA"), W("vN"), Op.add)
+        tt(W("D", 0, 44), W("LH", 0, 44), lr, Op.subtract)
+        tt(W("E", K, 2 * K), l, W("LH", K, 2 * K), Op.subtract)
+        fa, fb = W("F", K, 3 * K), W("F", 0, 2 * K)
+        n = [lambda: tt(W("N1", 0, 44), fa, W("Q", 0, 44), Op.mult), lambda: tt(W("N2", 0, 44), fb, W("SS", 0, 44), Op.mult),
+             lambda: tt(W("N3", 0, 44), W("N1", 0, 44), W("N2", 0, 44), Op.add), lambda: tt(W("N4", 0, 44), W("CB", 0, 44), W("N3", 0, 44), Op.add),
+             lambda: cp(U("SL%d" % j, 0, 44), W("N4", 0, 44))]
+        if j == 0:
+            n[0](), n[1]()
+        tt(W("M1", 0, 44), fa, W("D", 0, 44), Op.mult)
+        tt(W("M2", 0, 44), fb, W("E", 0, 44), Op.mult)
+        n[2 if j == 0 else 0]()
+        tt(W("M3", 0, 44), W("M1", 0, 44), W("M2", 0, 44), Op.add)
+        n[3 if j == 0 else 1]()
+        tt(ln, lr, W("M3", 0, 44), Op.add)
+        if j == 0:
+            n[4]()
+            cp(U("OL1"), W("LR1"))
+            tt(R("a1"), R("wa", 2 * C, 4 * C), R("sg1"), Op.add, sr)
+            tt(R("lrs"), R("wa", 0, 2 * C), R("a1"), Op.add, sl)
+        else:
+            n[2]()
+            cp(R("soR%d" % rd), ln)
+            n[3]()
+            n[4]()
+
+    for rd in range(3):
+        last = rd == 2
+        partner = T.cores[rank ^ STEP[rd]]
+        ra, rb, rc = route(topo, core, partner)
+
+        def to(relay, lo, n):
+            return bits(topo.engines(core, relay)[lo:lo + n])
+
+        def remote(buf, sem, relay, lo, n, a=0):
+            rid, pid = topo.addr(relay, core)
+            o, i = T["ro%s%d" % (buf, rd)], T["so%s%d" % (buf, rd)]
+            send([R("so%s%d" % (buf, rd))],
+                 lambda: g.remote_dma(o[:], i[:, a:], T.sem["a%s%d" % (sem, rd)], T.sem["ls"], pid, rid, to(relay, lo, n)), n)
+
+        scores(0, C if rd == 0 else HALF, 0)
+        if rd > 0:
+            signs(HALF, C, 2)
+        signs(0, C if rd == 0 else HALF, 0)
+
+        def more():
+            for t in range(0 if rd == 0 else 4):
+                act(R("win", 704 * t + C, 704 * t + C + HALF), R("ps%d" % (4 + t), 0, HALF), scale=0.5)
+            if rd == 0:
+                shift(R("sgt"), R("lrf"), 2.0 ** 12, -511.0 / 1024)
+                shift(R("a1"), R("sgt"), 1.0, 1.5 * 2.0 ** 23)
+                shift(R("sg1"), R("a1"), 1.0, -1.5 * 2.0 ** 23)
+                act(R("wa", 3 * C, 4 * C), R("sg1"), scale=FR * F10)
+                act(R("wa", C, 2 * C), R("sg1"), scale=FR)
+                replicas(2)
+            for k in range(2, 4):
+                mm(2 + k, "ur", 128 * k, "qx", "sx", 0, C)
+            act(R("sg1"), R("ps4", 0, C), func=Act.Sign, scale=-1.0)
+
+        def rest():
+            act(R("sgt"), R("ps5", 0, C), func=Act.Sign)
+            act(R("pf1", 0, C), R("sgt"), func=Act.Relu, scale=0.5)
+            act(R("pf1", C, 2 * C), R("sgt"), func=Act.Relu, scale=0.5)
+            act(R("tw1", 2 * C, 3 * C), R("none"), scale=0.0)
+            if not last:
+                act(R("pw0", 0, C), R("none"))
+        step(rd, 0, more, rest)
+        step(rd, 1)
+        remote("R", "R", ra, 0, sent_on("R", rd), K)
+        lists[0], lists[1] = R("soR%d" % rd, 0, K), R("soR%d" % rd, K, 2 * K)
+        part = lambda r, lo, hi: (r[0], r[1] + lo // 16, r[1] + hi // 16, 1)
+        for h, (lo, hi) in enumerate(CHUNKS):
+            for t in range(4):
+                if h == 0 and rd == 0:
+                    act(R("win", 704 * t + C, 704 * t + 2 * C), R("lvt", t, 4 * C, 4), scale=0.5)
+            if h == 0:
+                windows()
+            for t in range(4):
+                act(R("gl", C * t + lo, C * t + hi), R("win", 704 * t, 704 * t + 704), part(lists[0], lo, hi))
+                tt(R("zt", 4 * lo + t, 4 * hi, 4), R("win", 704 * t, 704 * t + 704), R("gl", C * t + lo, C * t + hi), Op.add, part(lists[1], lo, hi))
+            quant("z", "zt", lo, hi)
+            for b in range(4):
+                mm(4 * h + b, "w", 128 * b, "qz", "sz", lo, hi)
+        act(R("ll", 0, C), R("wb", 0, 2 * C), U("SL1", 0, K))
+        for h, (lo, hi) in enumerate(CHUNKS):
+            for b in range(4):
+                o, i = R("hp", C * b + lo, C * b + hi), R("ps%d" % (4 * h + b), 0, hi - lo)
+                if b % 2 == 0 or (h, b) == (1, 3):
+                    ts(o, i, 0.03125, Op.mult)
+                else:
+                    act(o, i, scale=0.03125)
+            if h == 0:
+                act(R("ll", C, 2 * C), R("ll", 0, C))
+        arrive("laR%d" % rd, "aR%d" % rd, 8)
+        tt(R("gg"), R("ll"), R("dm"), Op.mult, R("laR%d" % rd))
+        pick(R("e3"), R("gg"))
+        ts(W("mi"), ends("e3"), 2.0 ** 22, Op.mult)
+        ts(W("mt"), ends("e3"), float(C) * FR, Op.is_ge, -float(C), Op.mult)
+        tt(W("mm"), W("mi"), W("mt"), Op.add)
+        cp(U("MO"), W("mm"))
+        cp(R("soM%d" % rd), W("mm", 11, 22))
+        remote("M", "M", rc, 8, sent_on("M", rd))
+        for b in range(4):
+            o, i, n = R("gt", b, 4 * HALF, 4), R("hp", C * b, C * b + C), U("MO", 0, 11)
+            if b % 2 == 0:
+                cp(o, i, n)
+            else:
+                act(o, i, n)
+        q, s = "soQ%d" % rd, "soS%d" % rd
+        quant("", "gt", 0, HALF, q, s)
+
+        def codes():
+            tr = []
+            for relay, lo, e in ((ra, 0, 0), (rb, 88, 8)):
+                rid, pid = topo.addr(relay, core)
+                tr.append(RemoteDMATransfer(dst_ids=[DstId(rid=rid, pnc=pid)], dma_engine_mask=to(relay, e, 8), remote_sem=T.sem["aC%d" % rd],
+                                            src=T[q][:, lo:lo + 88].bitcast(dt.uint8), dst=T["roQ%d" % rd][:, lo:lo + 88].bitcast(dt.uint8)))
+            g.remote_dma_fused(tr, local_sem=T.sem["ls"])
+        send([R(q)], codes, 16)
+        remote("S", "S", rc, 0, sent_on("S", rd))
+        act(R("wa", C, 2 * C), R("wb"), U("SL1", K, 2 * K))
+        act(R("wa", 0, C), R("ll", 0, C))
+        if not last:
+            act(R("wa", 2 * C, 4 * C), R("wa", 0, 2 * C), scale=F10)
+            parents("pw0", lists[0], lambda: ts(W("t1"), W("LR0"), float(C), Op.is_ge, -float(C), Op.mult),
+                    lambda: tt(W("t2"), W("LR0"), W("t1"), Op.add))
+            cp(U("OLC0"), W("t2"))
+            tt(W("dlp"), W("LR0"), W("par"), Op.subtract)
+        if rd == 0:
+            quant("e", "et", 0, 512)
+        if not last:
+            tt(R("lrf"), R("wa", 0, C), R("wa", 3 * C, 4 * C), Op.add)
+        else:
+            act(R("gro"), R("wa", 0, 2 * C), scale=2.0 ** 22)
+            store("y", T["gr"][:, :], T["gro"][0:128:16, :], R("gro"))
+            quant("v", "vt", 0, 128)
+        arrive("laM%d" % rd, "aM%d" % rd, 8)
+        own = R("laM%d" % rd, 0, 11)
+        for b in range(4):
+            x = R("xt", 4 * HALF + b, 4 * C, 4)
+            tt(x, R("hp", C * b, C * b + C), x, Op.add, own)
+        quant("x", "xt", HALF, C)
+        if not last:
+            for b in range(4):
+                act(R("win", 704 * b + C + HALF, 704 * b + 2 * C), R("hp", C * b, C * b + C), own, scale=0.5)
+        else:
+            mm(0, "v", 0, "qx", "sx", HALF, C)
+            act(R("yo", HALF, C), R("ps0", 0, HALF))
+            store("y", T["oc"][:, 4 * HALF:4 * C], T["qx"][:, HALF:C].bitcast(dt.uint8), R("qx", HALF, C))
+            for k in range(4):
+                store("y", T["osc"][4 * k:4 * k + 4, HALF:C], T["sx"][32 * k:32 * k + 4, HALF:C], R("sx", HALF, C))
+            store("y", T["y"][:, HALF:C], T["yo"][:, HALF:C], R("yo", HALF, C))
+        arrive("laQ%d" % rd, "aC%d" % rd, 16)
+        arrive("laS%d" % rd, "aS%d" % rd, 8)
+        for b in range(4):
+            mm(4 + b, "e", 128 * b, "laQ%d" % rd, "laS%d" % rd, 0, HALF)
+        if not last:
+            scores(HALF, C, 2)
+        for b in range(4):
+            x = R("xt", b, 4 * HALF, 4)
+            tt(x, R("ps%d" % (4 + b), 0, HALF), x, Op.add)
+        quant("x", "xt", 0, HALF)
+    mm(1, "v", 0, "qx", "sx", 0, HALF)
+    act(R("yo", 0, HALF), R("ps1", 0, HALF))
+    store("y", T["oc"][:, 0:4 * HALF], T["qx"][:, 0:HALF].bitcast(dt.uint8), R("qx", 0, HALF))
+    for k in range(4):
+        store("s" if k % 2 else "y", T["osc"][4 * k:4 * k + 4, 0:HALF], T["sx"][32 * k:32 * k + 4, 0:HALF], R("sx", 0, HALF))
+    store("s", T["y"][:, 0:HALF], T["yo"][:, 0:HALF], R("yo", 0, HALF))
+    for s in sorted(count):
+        g.wait_ge(T.sem[s], count[s])

@@ -1,29 +1,16 @@
+import math
 from concourse.bass import DstId, RemoteDMATransfer
 from concourse.mybir import dt, AluOpType, ActivationFunctionType
 
 Op, Act = AluOpType, ActivationFunctionType
 C, HALF, K = 352, 176, 22
 STEP = [1, 2, 4]
-FR, F10 = 2.0 ** -22, 2.0 ** 10
 CHUNKS = [(0, 192), (192, 352)]
-WIDE = [("LR0", 44), ("LR1", 44), ("CB", 44), ("F", 66), ("LH", 44), ("D", 44), ("E", 44), ("Q", 44), ("SS", 44), ("M1", 44), ("M2", 44), ("M3", 44),
-        ("N1", 44), ("N2", 44), ("N3", 44), ("N4", 44), ("t1", 44), ("t2", 44), ("par", 22), ("x", 22), ("i32", 22), ("A", 22), ("dlp", 22), ("aM", 22),
-        ("o", 22), ("I", 22), ("vA", 22), ("vN", 22), ("mi", 22), ("mt", 22), ("mm", 22), ("c704", 22)]
-U16S = [("OLs", 44), ("OL1", 22), ("OLC0", 22), ("OLC1", 22), ("O", 22), ("SL0", 44), ("SL1", 44), ("LX", 22), ("MO", 22)]
-FTHS = [("tA", 22), ("tP", 22), ("tN", 22), ("tQ", 22), ("pk", 22), ("px", 8)]
-
-
-def places(blocks):
-    at, d = 0, {}
-    for n, w in blocks:
-        d[n] = at
-        at += (w + 7) // 8 * 8
-    return d, at
-
-
-WI, WIN_ = places(WIDE)
-WU, WUN = places(U16S)
-WF, WFN = places(FTHS)
+SENT = 34
+L, RT, ID, COL = 0, 4, 1, 2
+PAIRS = ["act", "acd", "at", "dt", "Dl", "Db", "E", "El", "Z", "m1", "m2", "m3", "m4", "m5", "la", "ra", "rb"]
+INTS = [("p", 8), ("a", 8), ("b", 8), ("c", 8), ("d", 8), ("e", 8), ("j", 8), ("q", 8), ("n", 48), ("lo", 48), ("m", 24), ("lw", 24), ("rw", 24)]
+COLS = ["sig", "mb", "k", "h", "pm", "p32", "f1", "nf", "n2"]
 
 
 def codes_of(name, n):
@@ -35,24 +22,24 @@ def tiles(kind, **widths):
 
 
 SCRATCH = {
-    **tiles("bfloat16", xt=4 * C, lvt=4 * C, ut=512, vt=512, win=8 * C, gl=4 * C, zt=4 * C, hp=4 * C, gt=4 * HALF, et=2048, one=512, kmb=C, e1b=C, e2b=C, e1s=C, e2s=C, twb=C, dmb=C),
-    **codes_of("x", C), **codes_of("u", 128), **codes_of("ur", 512), **codes_of("v", 128), **codes_of("w", 512), **codes_of("e", 512), **codes_of("z", C),
-    **tiles("int32", lw=K, rw=K, wi=WIN_, ui=32),
-    **tiles("uint16", wu=WUN, ux=32),
-    **tiles("float32", wf=WFN, ones=32, ex=704, tr=704, kr=C, dm=C, km=C, rc=C, none=C, wa=4 * C, wb=4 * C, lrf=C, lrs=C, a1=C, tw0=2 * C, tw1=4 * C,
-            pw0=2 * C, sg0=C, sg1=C, sgt=C, pf0=C, pf1=2 * C, e1=C, e2=C, gg=C, e3=C, gro=2 * C, yo=C, ll=2 * C),
+    **tiles("bfloat16", xt=4 * C, lvt=4 * C, ut=512, vt=512, win=8 * C, gl=4 * C, zt=4 * C, hp=4 * C, gt=4 * HALF, et=2048, one=512,
+            sg=2 * C, ga=2 * C, gb=C, gp=C, pw0=2 * C, pw1=2 * C, pre=C, zero=C, town=C, tga=C, tgb=C, tpu=C, t2=C, tab2=2 * C, tl=C, tabp=2 * C,
+            g1=208, g2=208, mt1=384, mt2=384, dq=88, pr=48 * len(PAIRS)),
+    **codes_of("x", C), **codes_of("u", 128), **codes_of("ur", 128), **codes_of("v", 128), **codes_of("w", 512), **codes_of("e", 512), **codes_of("z", C),
+    **{"i" + n: ("sbuf", [128, w], "int32") for n, w in INTS},
+    **tiles("uint16", ux=8, sel=4, ms=2, ol=32, op=32, mo1=16, mo2=16),
+    **tiles("float32", cols=24 * len(COLS), X=160, U=128, yo=C, grt=C, gro=C),
 }
 for _b in range(8):
     SCRATCH["ps%d" % _b] = ("psum", [128, 512], "float32")
 for _r in range(3):
     for _n in ("so", "ro", "la"):
-        SCRATCH["%sR%d" % (_n, _r)] = ("sbuf", [128, 2 * K if _n == "so" else K], "uint16")
-        SCRATCH["%sM%d" % (_n, _r)] = ("sbuf", [128, 11], "uint16")
+        SCRATCH["%sR%d" % (_n, _r)] = ("sbuf", [128, K + 48 if _n == "so" else SENT], "uint16")
         SCRATCH["%sQ%d" % (_n, _r)] = ("sbuf", [128, HALF], "float8_e4m3fn_x4")
         SCRATCH["%sS%d" % (_n, _r)] = ("sbuf", [128, HALF], "uint8")
 LOADS = ["lt", "rt", "x", "u", "lv", "wc", "ws", "v"]
-SEMAPHORES = (["cv", "cs", "ct", "cp", "ls", "outs"] + ["ld_" + n for n in LOADS]
-              + ["a%s%d" % (n, r) for n in "RMCS" for r in range(3)])
+SEMAPHORES = (["cv", "cs", "ct", "cp", "ls", "outs"] + ["ld_" + n for n in LOADS] + ["d%d" % n for n in range(12)]
+              + ["a%s%d" % (n, r) for n in "RCS" for r in range(3)])
 
 
 def route(topo, core, partner):
@@ -66,10 +53,6 @@ def bits(engines):
     return sum(1 << e for e in engines)
 
 
-def sent_on(kind, rd):
-    return 16 if kind == "S" or (kind == "R" and rd) else 8
-
-
 def relay_program(g, core, T, topo, rank):
     src, sent = T.cores[rank], 0
     for rd, s in enumerate(STEP):
@@ -79,9 +62,9 @@ def relay_program(g, core, T, topo, rank):
             continue
         rid, pid = topo.addr(dst, core)
         eng = topo.engines(core, dst)[:8]
-        jobs = {a: [("R", "R", 0, K), ("C", "Q", 0, 88)], b: [("C", "Q", 88, HALF)], c: [("M", "M", 0, 11), ("S", "S", 0, HALF)]}[core]
-        for sem, buf, lo, hi in jobs:
-            g.wait_ge(T.sem["a%s%d" % (sem, rd)], sent_on(sem, rd))
+        jobs = {a: [("C", "Q", 0, 88, 8)], b: [("C", "Q", 88, HALF, 8)], c: [("R", "R", 0, SENT, 16), ("S", "S", 0, HALF, 16)]}[core]
+        for sem, buf, lo, hi, n in jobs:
+            g.wait_ge(T.sem["a%s%d" % (sem, rd)], n)
             o, i = T["la%s%d" % (buf, rd)][:, lo:hi], T["ro%s%d" % (buf, rd)][:, lo:hi]
             if buf == "Q":
                 o, i = o.bitcast(dt.uint8), i.bitcast(dt.uint8)
@@ -105,11 +88,10 @@ def rank_program(g, core, T, topo):
     known = {q: {} for q in eng}
     uses = {}
     clocks = {}
+    moves = []
 
     def meet(a, b):
-        if a[1] >= b[2] or b[1] >= a[2]:
-            return False
-        return not (a[3] == b[3] and a[3] > 1 and (a[1] - b[1]) % a[3])
+        return not (a[1] >= b[2] or b[1] >= a[2] or (a[1] - b[1]) % math.gcd(a[3], b[3]))
 
     def before(q, reads, writes):
         need = {}
@@ -130,7 +112,7 @@ def rank_program(g, core, T, topo):
     def note(q, tok, reads, writes):
         clocks[tok] = dict(known[q])
         for r in writes:
-            uses[r[0]] = [u for u in uses.get(r[0], []) if not (r[3] in (1, u[0][3]) and r[1] <= u[0][1] and u[0][2] <= r[2] and (u[0][1] - r[1]) % r[3] == 0)]
+            uses[r[0]] = [u for u in uses.get(r[0], []) if not (u[0][3] % r[3] == 0 and r[1] <= u[0][1] and u[0][2] <= r[2] and (u[0][1] - r[1]) % r[3] == 0)]
         for w, regs in ((False, reads), (True, writes)):
             for r in regs:
                 uses.setdefault(r[0], []).append((r, w, q, tok))
@@ -152,17 +134,31 @@ def rank_program(g, core, T, topo):
         eng[q].dma_start(out, in_).then_inc(T.sem["outs"], 16)
         count["outs"] += 16
 
+    def move(out, in_):
+        before("y", [in_], [out])
+        s = "d%d" % len(moves)
+        moves.append(s)
+        g.sync.dma_start(ap(out), ap(in_)).then_inc(T.sem[s], 16)
+        count[s] = 16
+        note("y", (s, 16), [in_], [out])
+
     def R(name, lo=0, hi=None, step=1):
         return (name, lo, SCRATCH[name][1][1] if hi is None else hi, step)
 
-    def W(name, lo=0, hi=K):
-        return ("wi", WI[name] + lo, WI[name] + hi, 1)
+    def I(name, lo=0, hi=None):
+        return R("i" + name, lo, hi)
 
-    def U(name, lo=0, hi=K):
-        return ("wu", WU[name] + lo, WU[name] + hi, 1)
+    def col(name, n=1):
+        return R("cols", 24 * COLS.index(name), 24 * COLS.index(name) + n)
 
-    def Fl(name, lo=0, hi=K):
-        return ("wf", WF[name] + lo, WF[name] + hi, 1)
+    def P(name):
+        return R("pr", 48 * PAIRS.index(name), 48 * PAIRS.index(name) + 2 * K)
+
+    def pair(name, f):
+        return (name, f, C, 8)
+
+    def field(name, f):
+        return (name, f, C, 16)
 
     def ap(r):
         return T[r[0]][:, r[1]:r[2]] if r[3] == 1 else T[r[0]][:, r[1]:r[2]:r[3]]
@@ -171,16 +167,19 @@ def rank_program(g, core, T, topo):
         return ap(r) if ind is None else ap(r).indirect(ap(ind))
 
     def given(*rs):
-        return [r for r in rs if r is not None]
+        return [r for r in rs if isinstance(r, tuple)]
+
+    def num(s):
+        return ap(s) if isinstance(s, tuple) else s
 
     def tt(out, in0, in1, op, ind=None):
         run("v", lambda: g.vector.tensor_tensor(ap(out), src(in0, ind), ap(in1), op), given(in0, in1, ind), [out])
 
-    def ts(out, in0, s1, op0, s2=None, op1=None):
+    def ts(out, in0, s1, op0, s2=None, op1=None, ind=None):
         if op1 is None:
-            run("v", lambda: g.vector.tensor_scalar(ap(out), ap(in0), s1, None, op0), [in0], [out])
+            run("v", lambda: g.vector.tensor_scalar(ap(out), src(in0, ind), num(s1), None, op0), given(in0, s1, ind), [out])
         else:
-            run("v", lambda: g.vector.tensor_scalar(ap(out), ap(in0), s1, s2, op0, op1), [in0], [out])
+            run("v", lambda: g.vector.tensor_scalar(ap(out), src(in0, ind), num(s1), num(s2), op0, op1), given(in0, s1, s2, ind), [out])
 
     def cp(out, in_, ind=None):
         run("v", lambda: g.vector.tensor_copy(ap(out), src(in_, ind)), given(in_, ind), [out])
@@ -191,17 +190,17 @@ def rank_program(g, core, T, topo):
     def fill(out, c):
         run("v", lambda: g.vector.memset(ap(out), c), [], [out])
 
+    def turn(out, in_):
+        run("v", lambda: g.vector.transpose(ap(out), ap(in_)), [in_], [out])
+
     def act(out, in_, ind=None, func=Act.Copy, scale=1.0):
         if scale == 1.0:
             run("s", lambda: g.scalar.activation(ap(out), src(in_, ind), func), given(in_, ind), [out])
         else:
-            run("s", lambda: g.scalar.activation(ap(out), src(in_, ind), func, scale=scale), given(in_, ind), [out])
+            run("s", lambda: g.scalar.activation(ap(out), src(in_, ind), func, scale=num(scale)), given(in_, ind, scale), [out])
 
     def shift(out, in_, scale, bias):
-        run("s", lambda: g.scalar.activation(ap(out), ap(in_), Act.Identity, bias=bias, scale=scale), [in_], [out])
-
-    def scan(out, d0, d1, op0, op1):
-        run("v", lambda: g.vector.tensor_tensor_scan(ap(out), ap(d0), ap(d1), 0.0, op0, op1), [d0, d1], [out])
+        run("s", lambda: g.scalar.activation(ap(out), ap(in_), Act.Identity, bias=num(bias), scale=scale), given(in_, bias), [out])
 
     def quant(name, tile, lo, hi, q=None, s=None):
         q, s = q or "q" + name, s or "s" + name
@@ -222,29 +221,21 @@ def rank_program(g, core, T, topo):
         fn()
         count["ls"] += n
 
-    def masked(out, row):
-        scan(out, row, R("dm"), Op.add, Op.mult)
-
-    def pick(out, row):
-        scan(out, R("km"), row, Op.mult, Op.add)
-
-    def ends(name):
-        return (name, 15, C, 16)
-
-    def col16(out, x):
-        w = x[2] - x[1]
-        ts(W("t1", 0, w), x, float(C), Op.is_ge, -float(C), Op.mult)
-        tt(W("t2", 0, w), x, W("t1", 0, w), Op.add)
-        cp(out, W("t2", 0, w))
-
     def iota(out, pattern, base, cm):
-        if out[0] in ("kr", "rc"):
-            run("p", lambda: g.iota(ap(out), pattern, base, cm, allow_small_or_imprecise_dtypes=True), [], [out])
-        else:
-            run("p", lambda: g.iota(ap(out), pattern, base, cm), [], [out])
+        run("p", lambda: g.iota(ap(out), pattern, base, cm), [], [out])
 
-    load("y", "ld_lt", T["lw"][:], T["lt"][:], R("lw"))
-    load("s", "ld_rt", T["rw"][:], T["rt"][:], R("rw"))
+    def swap(n, *between):
+        for k in range(2 * n):
+            turn(R("U", 32 * k, 32 * k + 32), R("X", 32 * (k // 2), 32 * (k // 2) + 32))
+        for f in between:
+            f()
+        turn(R("X", 64, 64 * n + 32), R("U", 16, 64 * n - 16))
+
+    def name(k, buf, f):
+        tt(R("X", 32 * k, 32 * k + K), field(buf, f), field(buf, f + 8), Op.add)
+
+    load("y", "ld_lt", T["ilw"][:, 0:K], T["lt"][:], I("lw"))
+    load("s", "ld_rt", T["irw"][:, 0:K], T["rt"][:], I("rw"))
     load("y", "ld_u", T["ut"][:], T["u"][:], R("ut"))
     load("s", "ld_x", T["xt"][:], T["x"][:], R("xt"))
     load("y", "ld_lv", T["lvt"][:], T["lv"][:], R("lvt"))
@@ -252,263 +243,223 @@ def rank_program(g, core, T, topo):
     load("y", "ld_ws", T["sw"][:, 0:512], T["ws"][:, 0:512], R("sw"))
     load("y", "ld_v", T["vt"][:], T["v"][:], R("vt"))
 
-    iota(W("x"), [[0, K]], 0, 1)
-    iota(R("kr"), [[0, K], [1, 16]], 0, 0)
-    iota(W("i32"), [[32, K]], 0, 0)
-    iota(W("mm"), [[16, K]], 0, 0)
-    iota(R("ui"), [[1, 4], [16, 8]], 0, 0)
-    iota(R("rc"), [[1, C]], 0, 0)
-    fill(R("none"), float(C))
-    fill(R("ones"), 1.0)
-    fill(R("km"), 1.0)
-    fill(W("SS"), C)
-    ts(W("t1"), W("x"), 31, Op.bitwise_and)
-    ts(W("t2"), W("x"), 15, Op.bitwise_and)
-    fill(R("km", 0, C, 16), 0.0)
-    act(R("pw0", 0, C), R("none"))
-    act(R("tw0", C, 2 * C), R("none"), scale=0.0)
-    act(R("tw1", C, 2 * C), R("none"), scale=0.0)
-    act(R("kmb"), R("km"))
-    act(R("wb", 2 * C, 3 * C), R("none"), scale=0.0)
-    cp(Fl("px", 0, 8), W("t2", 0, 8))
-    tt(W("mt"), W("t1"), W("i32"), Op.add)
-    px = Fl("px", 0, 1)
-    shift(R("one", 0, C), R("none"), 0.0, 1.0)
-    shift(R("one", C, 512), R("none", 0, 160), 0.0, 1.0)
-    run("v", lambda: g.vector.tensor_scalar(T["dm"][:], T["kr"][:], ap(px), None, Op.is_equal), [R("kr"), px], [R("dm")])
-    act(R("dmb"), R("dm"))
-    cp(U("LX"), W("mt"))
-    tt(W("CB"), W("t2"), W("mm"), Op.add)
-    cp(R("ux"), R("ui"))
-    ts(W("CB", K, 2 * K), W("CB"), float(C), Op.add)
-    ts(W("c704"), W("CB"), 2.0 * C, Op.add)
+    iota(I("p"), [[0, 8]], 0, 1)
+    iota(I("j"), [[16, 8]], 0, 0)
+    iota(I("m", 0, K), [[32, 11], [0, 2]], 0, 0)
+    fill(R("X"), 0.0)
+    fill(R("zero"), 0.0)
+    fill(R("one"), 1.0)
+    ts(I("a"), I("p"), 15, Op.bitwise_and)
+    ts(I("b"), I("p"), 4, Op.arith_shift_right, 1, Op.bitwise_and)
+    ts(I("c"), I("p"), 3, Op.bitwise_and)
+    ts(I("d"), I("p"), 1, Op.arith_shift_right, 2, Op.bitwise_and)
+    ts(I("e"), I("p"), 31, Op.bitwise_and)
+    tt(I("q"), I("a"), I("j"), Op.add)
+    cp(col("h"), I("b", 0, 1))
+    ts(col("mb"), I("c", 0, 1), 3.0, Op.is_equal)
+    ts(col("nf"), I("c", 0, 1), 2.0, Op.is_equal, -2.0, Op.mult)
+    ts(col("n2"), I("c", 0, 1), 0.0, Op.is_gt)
+    ts(col("f1"), I("a", 0, 1), float(ID), Op.is_equal, float(C), Op.mult)
+    cp(col("p32"), I("e", 0, 1))
+    ts(I("e"), I("q"), float(K), Op.is_ge)
+    tt(col("k"), col("mb"), I("d", 0, 1), Op.add)
+    tt(col("sig"), col("nf"), col("n2"), Op.add)
+    ts(I("c"), I("e"), -float(K), Op.mult)
+    ts(R("ux"), I("j"), col("k"), Op.add)
+    tt(I("q"), I("q"), I("c"), Op.add)
+    ts(I("d"), I("e"), 32.0, Op.mult, col("h"), Op.add)
+    ts(I("e"), I("e"), 32.0, Op.mult, 64.0, Op.add)
+    ts(I("c"), I("q"), 1, Op.bitwise_and)
+    ts(I("q"), I("q"), 62, Op.bitwise_and)
+    ts(I("c"), I("c"), col("h"), Op.not_equal)
+    tt(I("q"), I("q"), I("d"), Op.add)
+    tt(I("c"), I("c"), I("e"), Op.mult)
+    quant("u", "ut", 0, 128)
+    tt(I("q"), I("q"), I("c"), Op.add)
+    cp(R("X", 0, K), I("rw", 0, K))
+    cp(R("X", 32, 32 + K), I("lw", 0, K))
+    cp(R("sel"), I("q", 0, 4))
 
-    ts(W("mi"), R("rw"), 1024.0, Op.mult)
-    cp(U("OLs"), R("lw"))
-    tt(Fl("pk"), W("mi"), R("lw"), Op.add)
-    for q in range(K):
-        o, i = R("ex", 32 * q, 32 * q + 32), Fl("pk", q, q + 1)
-        run("s", lambda: g.scalar.activation(ap(o), T["ones"][:], Act.Copy, scale=ap(i)), [R("ones"), i], [o])
+    def replicas():
+        run("v", lambda: g.vector.tensor_copy(T["qur"][:].bitcast(dt.uint32), T["qu"][:].bitcast(dt.uint32).indirect(T["ux"][:])),
+            [R("qu"), R("ux")], [R("qur")])
+        run("s", lambda: g.scalar.activation(T["sur"][:], T["su"][:].indirect(T["ux"][:]), Act.Copy), [R("su"), R("ux")], [R("sur")])
 
-    def replicas(k):
-        a, e = 128 * k, 8 * k
-        run("v", lambda: g.vector.tensor_copy(T["qur"][:, a:a + 256].bitcast(dt.uint32), T["qu"][:, 0:128].bitcast(dt.uint32).indirect(T["ux"][:, e:e + 16])),
-            [R("qu"), R("ux")], [R("qur", a, a + 256)])
-        run("s", lambda: g.scalar.activation(T["sur"][:, a:a + 256], T["su"][:, 0:128].indirect(T["ux"][:, e:e + 16]), Act.Copy),
-            [R("su"), R("ux")], [R("sur", a, a + 256)])
-
-    def parents(pw, ol, *between):
-        f = list(between) + [lambda: None] * 2
-        put(R(pw), ol, R("rc"))
-        f[0]()
-        masked(R("e1"), R(pw, 0, C))
-        f[1]()
-        pick(R("e2"), R("e1"))
-        cp(W("par"), ends("e2"))
-
-    def start():
-        quant("u", "ut", 0, 128)
-        replicas(0)
-
-    lists = [U("OLs"), None]
-    parents("pw0", lists[0], start)
+    swap(2, replicas)
+    cp(R("ol", 0, K), I("lw", 0, K))
+    cp(I("n"), R("X"), R("sel", 0, 3))
     quant("x", "xt", 0, C)
-    run("v", lambda: g.vector.transpose(T["tr"][:], T["ex"][:]), [R("ex")], [R("tr")])
-    act(R("lrf"), R("tr"), U("LX"), scale=FR)
-    cp(W("LR0"), R("lw"))
-    cp(W("LR0", K, 2 * K), R("rw"))
-    col16(U("OLC0"), W("LR0"))
-    tt(W("dlp"), W("LR0"), W("par"), Op.subtract)
+    ts(I("lo"), I("n"), 31, Op.bitwise_and)
+    act(R("pw0", 0, C), R("zero"))
+    act(R("ga", C, 2 * C), R("zero"))
+    mm(0, "ur", 0, "qx", "sx", 0, C)
+    for f, at in ((0, K), (1, 0)):
+        tt(R("dq", f, 88, 4), I("n", at, at + K), I("lo", at, at + K), Op.subtract)
+        cp(R("dq", 2 + f, 88, 4), I("lo", at, at + K))
     for b in range(4):
         run("p", lambda: g.affine_select(T["et"][:, 512 * b:512 * b + 512], T["one"][:], [[-1, 512]], Op.is_equal, 0.0, b, 4),
             [R("one")], [R("et", 512 * b, 512 * b + 512)])
 
-    def windows():
-        for t in range(4):
-            act(R("win", 704 * t, 704 * t + C), R("xt", t, 4 * C, 4), scale=0.5)
+    def flags(bank, lo, hi):
+        ts(R("sg", lo, hi), R("ps%d" % bank, 0, hi - lo), col("sig"), Op.mult, 0.0, Op.is_gt)
+        act(R("sg", C + lo, C + hi), R("ps%d" % bank, 0, hi - lo), func=Act.Sign, scale=col("mb"))
 
-    def scores(lo, hi, bank):
-        for k in range(2):
-            mm(bank + k, "ur", 128 * k, "qx", "sx", lo, hi)
-        act(R("sg0", lo, hi), R("ps%d" % bank, 0, hi - lo), func=Act.Sign, scale=-1.0)
+    def plane(t, lo, hi):
+        act(R("win", 704 * t + lo, 704 * t + hi), R("xt", 4 * lo + t, 4 * hi, 4), scale=0.5)
 
-    def signs(lo, hi, bank):
-        ts(R("pf0", lo, hi), R("ps%d" % (bank + 1), 0, hi - lo), 0.0, Op.is_gt, 0.5, Op.mult)
-        scan(R("e1s", lo, hi), R("ps%d" % bank, 0, hi - lo), R("dm", lo, hi), Op.add, Op.mult)
-        tt(R("lrs", lo, hi), R("lrf", lo, hi), R("sg0", lo, hi), Op.add)
-        scan(R("e2s", lo, hi), R("kmb", lo, hi), R("e1s", lo, hi), Op.mult, Op.add)
-        ts(W("A", lo // 16, hi // 16), ("e2s", lo + 15, hi, 16), 0.0, Op.is_gt)
+    def differences(own):
+        l, r = pair(own, L), pair(own, RT)
+        tt(P("Dl"), pair("tga", L), l, Op.subtract)
+        tt(P("Db"), pair("tga", RT), r, Op.subtract)
+        tt(P("E"), l, pair("tga", RT), Op.subtract)
 
-    def step(rd, j, more=None, rest=None):
-        lr, ln = W("LR%d" % j, 0, 44), W("LR%d" % (1 - j), 0, 44)
-        l, r = W("LR%d" % j), W("LR%d" % j, K, 2 * K)
-        tw, pf = "tw%d" % j, R("pf%d" % j)
-        sl, sr = U("SL0", 0, K), U("SL0", K, 2 * K)
-        if j == 0:
-            tt(R(tw, 0, C), pf, R("lrs"), Op.add, U("OLC0"))
-            act(R("twb"), R(tw, 0, C))
-            more()
+    def step(j, own, out, ready, pw, gap):
+        l, r = pair(own, L), pair(own, RT)
+        ol = R("ol", 0, K)
+        pos, neg, way = 1 + 4 * j, 2 + 4 * j, 3 + 4 * j
+        act(R("ga", 0, C), R("sg"), ol, func=Act.Relu)
+        act(R("gb"), R("ga"), ol)
+        gap()
+        if ready:
+            cp(R("gp"), R("sg"), R("op", 0, K))
+            turn(R("town"), R("sg", 0, C))
+            turn(R("tga"), R("ga", 0, C))
+            turn(R("tpu"), R("gp"))
         else:
-            tt(R(tw, 0, C), pf, R("lrs"), Op.add, U("OL1"))
-            act(R("twb"), R(tw, 0, C))
-            act(R("wb", 0, C), R("wa", 0, 2 * C), sl)
-            act(R("wb", C, 2 * C), R("wa", 0, 2 * C), sr)
-        own = ends("e2b")
+            tt(P("El"), r, l, Op.subtract)
+            put(R(pw), ol, R("sg", 0, C))
+            turn(R("tga"), R("ga", 0, C))
+            turn(R("tpu"), R(pw, 0, C))
+            turn(R("tgb"), R("gb"))
+            differences(own)
+            tt(P("Z"), pair("tpu", RT), r, Op.subtract)
+        tt(P("act"), pair("town", pos), pair("tga", neg), Op.mult)
+        tt(P("acd"), pair("town", neg), pair("tpu", pos), Op.mult)
+        late = lambda: tt(P("at"), P("act"), pair("tgb", way), Op.mult)
+        if not ready:
+            late()
+        tt(P("m5"), P("act"), P("Db"), Op.mult)
+        tt(P("dt"), P("acd"), pair("tga", way), Op.mult)
+        tt(P("m4"), P("acd"), P("Z"), Op.mult)
+        if ready:
+            turn(R("tgb"), R("gb"))
+        tt(P("ra"), r, P("m5"), Op.add)
+        tt(P("m2"), P("dt"), P("El"), Op.mult)
+        if ready:
+            late()
+        tt(P("rb"), P("ra"), P("m4"), Op.add)
+        tt(P("la"), l, P("m2"), Op.add)
+        tt(P("m1"), P("at"), P("Dl"), Op.mult)
+        tt(P("m3"), P("at"), P("E"), Op.mult)
+        tt(pair(out, L), P("la"), P("m1"), Op.add)
+        tt(pair(out, RT), P("rb"), P("m3"), Op.add)
 
-        def ownmask():
-            scan(R("e1b"), R("twb"), R("dmb"), Op.add, Op.mult)
-
-        def picked():
-            scan(R("e2b"), R("kmb"), R("e1b"), Op.mult, Op.add)
-
-        if j == 1:
-            put(R(tw, 2 * C, 4 * C), U("OL1"), R("a1"))
-            shift(R("wb", 3 * C, 4 * C), R(tw, 2 * C, 3 * C), 1.0 / F10, 1.0 / F10)
-            ownmask()
-            tt(W("dlp"), l, W("c704"), Op.subtract)
-            picked()
-            tt(W("E"), r, l, Op.subtract)
-            ts(W("A"), own, 0.0, Op.is_lt)
-            tt(W("Q"), l, W("CB"), Op.subtract)
-        tt(W("aM"), W("A"), W("dlp"), Op.mult)
-        if j == 0:
-            tt(W("E"), r, l, Op.subtract)
-        tt(W("o"), W("aM"), W("par") if j == 0 else W("c704"), Op.add)
-        if j == 0:
-            tt(W("Q"), l, W("CB"), Op.subtract)
-        cp(U("O"), W("o"))
-        tt(R("gg"), R(tw, 0, (2 if j == 0 else 3) * C), R("dm"), Op.mult, U("O"))
-        tt(W("Q", K, 2 * K), W("o"), W("CB"), Op.subtract)
-        oth = ends("e3")
-        if j == 0:
-            ownmask()
-            pick(R("e3"), R("gg"))
-            picked()
-            ts(W("I"), oth, 1.0, Op.add, 2.0 ** 22, Op.mult)
-        ts(Fl("tP"), own, 0.0, Op.is_ge, 1.5, Op.add)
-        ts(Fl("tA"), own, 0.0, Op.is_ge, 1.0, Op.add)
-        ts(Fl("tN"), own, 1.0, Op.is_ge, -1.0, Op.add)
-        ts(Fl("tQ"), own, 1.5, Op.is_ge, -1.0, Op.add)
-        if j == 0:
-            if rd == 0:
-                tt(R("wa", 0, C), R("lrf"), R("wa", 3 * C, 4 * C), Op.subtract)
-                act(R("wa", 2 * C, 3 * C), R("wa", 0, C), scale=F10)
-            rest()
-        else:
-            pick(R("e3"), R("gg"))
-        ts(W("SS", K, 2 * K), W("Q", K, 2 * K), -1.0, Op.mult, -float(C), Op.add)
-        if j == 1:
-            ts(W("I"), oth, 1.0, Op.add, 2.0 ** 22, Op.mult)
-        tt(W("vA"), oth, Fl("tA"), Op.is_ge)
-        tt(W("vN"), oth, Fl("tN"), Op.is_lt)
-        ts(W("LH"), W("I"), 1023, Op.bitwise_and)
-        ts(W("LH", K, 2 * K), W("I"), 10, Op.arith_shift_right, 1023, Op.bitwise_and)
-        tt(W("F", K, 2 * K), oth, Fl("tP"), Op.is_ge)
-        tt(W("F"), oth, Fl("tQ"), Op.is_lt)
-        tt(W("F", 2 * K, 3 * K), W("vA"), W("vN"), Op.add)
-        tt(W("D", 0, 44), W("LH", 0, 44), lr, Op.subtract)
-        tt(W("E", K, 2 * K), l, W("LH", K, 2 * K), Op.subtract)
-        fa, fb = W("F", K, 3 * K), W("F", 0, 2 * K)
-        n = [lambda: tt(W("N1", 0, 44), fa, W("Q", 0, 44), Op.mult), lambda: tt(W("N2", 0, 44), fb, W("SS", 0, 44), Op.mult),
-             lambda: tt(W("N3", 0, 44), W("N1", 0, 44), W("N2", 0, 44), Op.add), lambda: tt(W("N4", 0, 44), W("CB", 0, 44), W("N3", 0, 44), Op.add),
-             lambda: cp(U("SL%d" % j, 0, 44), W("N4", 0, 44))]
-        if j == 0:
-            n[0](), n[1]()
-        tt(W("M1", 0, 44), fa, W("D", 0, 44), Op.mult)
-        tt(W("M2", 0, 44), fb, W("E", 0, 44), Op.mult)
-        n[2 if j == 0 else 0]()
-        tt(W("M3", 0, 44), W("M1", 0, 44), W("M2", 0, 44), Op.add)
-        n[3 if j == 0 else 1]()
-        tt(ln, lr, W("M3", 0, 44), Op.add)
-        if j == 0:
-            n[4]()
-            cp(U("OL1"), W("LR1"))
-            tt(R("a1"), R("wa", 2 * C, 4 * C), R("sg1"), Op.add, sr)
-            tt(R("lrs"), R("wa", 0, 2 * C), R("a1"), Op.add, sl)
-        else:
-            n[2]()
-            cp(R("soR%d" % rd), ln)
-            n[3]()
-            n[4]()
+    def unwrap(k, tab, lst):
+        gk, mt = "g%d" % k, "mt%d" % k
+        return [lambda: act(R(gk, 16, 192), R(tab), lst),
+                lambda: turn(R(mt, 0, 192), R(gk, 16, 208)), lambda: turn(R(mt, 192, 384), R(gk, 0, 192)),
+                lambda: ts(R("mo%d" % k, 0, 16), R(mt), float(HALF), Op.add, ind=R("ms", 0, 1))]
 
     for rd in range(3):
         last = rd == 2
         partner = T.cores[rank ^ STEP[rd]]
         ra, rb, rc = route(topo, core, partner)
+        so, la = "soR%d" % rd, "laR%d" % rd
 
         def to(relay, lo, n):
             return bits(topo.engines(core, relay)[lo:lo + n])
 
-        def remote(buf, sem, relay, lo, n, a=0):
+        def remote(buf, relay, n):
             rid, pid = topo.addr(relay, core)
             o, i = T["ro%s%d" % (buf, rd)], T["so%s%d" % (buf, rd)]
-            send([R("so%s%d" % (buf, rd))],
-                 lambda: g.remote_dma(o[:], i[:, a:], T.sem["a%s%d" % (sem, rd)], T.sem["ls"], pid, rid, to(relay, lo, n)), n)
+            send([R("so%s%d" % (buf, rd), 0, n)],
+                 lambda: g.remote_dma(o[:], i[:, 0:n], T.sem["a%s%d" % (buf, rd)], T.sem["ls"], pid, rid, to(relay, 0, 16)), 16)
 
-        scores(0, C if rd == 0 else HALF, 0)
-        if rd > 0:
-            signs(HALF, C, 2)
-        signs(0, C if rd == 0 else HALF, 0)
+        if rd == 0:
+            flags(0, 0, C)
+            turn(R("town"), R("sg", 0, C))
+            ts(I("c"), I("a"), col("h"), Op.add)
+            cp(R("town", 0, C, 4), R("dq"))
+            ts(I("d"), I("a"), 16.0, Op.mult, float(COL), Op.add)
+            turn(R("sg", 0, C), R("town"))
+            ts(I("c"), I("c"), 1, Op.bitwise_and)
+        else:
+            mm(0, "ur", 0, "qx", "sx", 0, HALF)
+            flags(0, 0, HALF)
 
-        def more():
-            for t in range(0 if rd == 0 else 4):
-                act(R("win", 704 * t + C, 704 * t + C + HALF), R("ps%d" % (4 + t), 0, HALF), scale=0.5)
+        def gap0():
             if rd == 0:
-                shift(R("sgt"), R("lrf"), 2.0 ** 12, -511.0 / 1024)
-                shift(R("a1"), R("sgt"), 1.0, 1.5 * 2.0 ** 23)
-                shift(R("sg1"), R("a1"), 1.0, -1.5 * 2.0 ** 23)
-                act(R("wa", 3 * C, 4 * C), R("sg1"), scale=FR * F10)
-                act(R("wa", C, 2 * C), R("sg1"), scale=FR)
-                replicas(2)
-            for k in range(2, 4):
-                mm(2 + k, "ur", 128 * k, "qx", "sx", 0, C)
-            act(R("sg1"), R("ps4", 0, C), func=Act.Sign, scale=-1.0)
+                act(R("pw1", 0, C), R("zero"))
+                for t in range(3):
+                    plane(t, 0, C)
+            else:
+                for t in range(4):
+                    act(R("win", 704 * t + C, 704 * t + C + HALF), R("ps%d" % (4 + t), 0, HALF), scale=0.5)
+                for t in range(2):
+                    plane(t, 0, HALF)
 
-        def rest():
-            act(R("sgt"), R("ps5", 0, C), func=Act.Sign)
-            act(R("pf1", 0, C), R("sgt"), func=Act.Relu, scale=0.5)
-            act(R("pf1", C, 2 * C), R("sgt"), func=Act.Relu, scale=0.5)
-            act(R("tw1", 2 * C, 3 * C), R("none"), scale=0.0)
-            if not last:
-                act(R("pw0", 0, C), R("none"))
-        step(rd, 0, more, rest)
-        step(rd, 1)
-        remote("R", "R", ra, 0, sent_on("R", rd), K)
-        lists[0], lists[1] = R("soR%d" % rd, 0, K), R("soR%d" % rd, K, 2 * K)
+        def gap1():
+            if rd == 0:
+                plane(3, 0, C)
+                for t in range(4):
+                    act(R("win", 704 * t + C, 704 * t + 2 * C), R("lvt", t, 4 * C, 4), scale=0.5)
+            else:
+                for t in range(2, 4):
+                    plane(t, 0, HALF)
+
+        step(0, "town" if rd == 0 else "t2", "town", rd > 0, "pw0", gap0)
+        name(0, "town", L)
+        swap(1, lambda: turn(R("sg", 0, C), R("town")))
+        if rd == 0:
+            fill(R("t2"), 0.0)
+        cp(R("ol"), R("X"), R("sel", 0, 2))
+        if rd == 0:
+            ts(I("c"), I("c"), 208.0, Op.mult)
+            cp(field("t2", ID), I("m", 0, K))
+            ts(field("t2", ID + 8), R("zero", 0, K), col("p32"), Op.add)
+            tt(I("c"), I("c"), I("d"), Op.add)
+            ts(R("ms"), I("c", 0, 2), 383.0, Op.min)
+        step(1, "town", "t2", False, "pw1", gap1)
+        name(0, "t2", RT)
+        name(1, "t2", L)
+        nl = R("X", 32, 32 + K)
+        swap(2, lambda: ts(col("nf", K), nl, float(C), Op.is_ge, -float(C), Op.mult))
+        tt(col("n2", K), nl, col("nf", K), Op.add)
+        cp(R(so, K, K + 48), R("X"), R("sel", 0, 3))
+        cp(R(so, 0, K), col("n2", K))
+        remote("R", rc, SENT)
+        ts(field("t2", COL), col("n2", K), -float(HALF), Op.add)
+        lr, ll = R(so, K, 2 * K), R(so, 2 * K, 3 * K)
         part = lambda r, lo, hi: (r[0], r[1] + lo // 16, r[1] + hi // 16, 1)
+        turn(R("tab2", 0, C), R("t2"))
+        move(R("tab2", C, 2 * C), R("tab2", 0, C))
+        if not last:
+            move(R("pw1", 0, C), R("zero"))
         for h, (lo, hi) in enumerate(CHUNKS):
             for t in range(4):
-                if h == 0 and rd == 0:
-                    act(R("win", 704 * t + C, 704 * t + 2 * C), R("lvt", t, 4 * C, 4), scale=0.5)
-            if h == 0:
-                windows()
-            for t in range(4):
-                act(R("gl", C * t + lo, C * t + hi), R("win", 704 * t, 704 * t + 704), part(lists[0], lo, hi))
-                tt(R("zt", 4 * lo + t, 4 * hi, 4), R("win", 704 * t, 704 * t + 704), R("gl", C * t + lo, C * t + hi), Op.add, part(lists[1], lo, hi))
+                act(R("gl", C * t + lo, C * t + hi), R("win", 704 * t, 704 * t + 704), part(ll, lo, hi))
+                tt(R("zt", 4 * lo + t, 4 * hi, 4), R("win", 704 * t, 704 * t + 704), R("gl", C * t + lo, C * t + hi), Op.add, part(lr, lo, hi))
             quant("z", "zt", lo, hi)
             for b in range(4):
                 mm(4 * h + b, "w", 128 * b, "qz", "sz", lo, hi)
-        act(R("ll", 0, C), R("wb", 0, 2 * C), U("SL1", 0, K))
+        if rd == 0:
+            fill(R("g1"), 0.0)
+            fill(R("g2"), 0.0)
+        arrive(la, "aR%d" % rd, 8)
+        m1 = unwrap(1, "tab2", R(la, K, K + 11))
         for h, (lo, hi) in enumerate(CHUNKS):
+            if h == 1:
+                m1[0]()
             for b in range(4):
                 o, i = R("hp", C * b + lo, C * b + hi), R("ps%d" % (4 * h + b), 0, hi - lo)
-                if b % 2 == 0 or (h, b) == (1, 3):
+                if h == 1 and b < 3:
                     ts(o, i, 0.03125, Op.mult)
                 else:
                     act(o, i, scale=0.03125)
-            if h == 0:
-                act(R("ll", C, 2 * C), R("ll", 0, C))
-        arrive("laR%d" % rd, "aR%d" % rd, 8)
-        tt(R("gg"), R("ll"), R("dm"), Op.mult, R("laR%d" % rd))
-        pick(R("e3"), R("gg"))
-        ts(W("mi"), ends("e3"), 2.0 ** 22, Op.mult)
-        ts(W("mt"), ends("e3"), float(C) * FR, Op.is_ge, -float(C), Op.mult)
-        tt(W("mm"), W("mi"), W("mt"), Op.add)
-        cp(U("MO"), W("mm"))
-        cp(R("soM%d" % rd), W("mm", 11, 22))
-        remote("M", "M", rc, 8, sent_on("M", rd))
+        for f in m1[1:]:
+            f()
         for b in range(4):
-            o, i, n = R("gt", b, 4 * HALF, 4), R("hp", C * b, C * b + C), U("MO", 0, 11)
+            o, i, n = R("gt", b, 4 * HALF, 4), R("hp", C * b, C * b + C), R("mo1", 0, 11)
             if b % 2 == 0:
                 cp(o, i, n)
             else:
@@ -524,45 +475,76 @@ def rank_program(g, core, T, topo):
                                             src=T[q][:, lo:lo + 88].bitcast(dt.uint8), dst=T["roQ%d" % rd][:, lo:lo + 88].bitcast(dt.uint8)))
             g.remote_dma_fused(tr, local_sem=T.sem["ls"])
         send([R(q)], codes, 16)
-        remote("S", "S", rc, 0, sent_on("S", rd))
-        act(R("wa", C, 2 * C), R("wb"), U("SL1", K, 2 * K))
-        act(R("wa", 0, C), R("ll", 0, C))
-        if not last:
-            act(R("wa", 2 * C, 4 * C), R("wa", 0, 2 * C), scale=F10)
-            parents("pw0", lists[0], lambda: ts(W("t1"), W("LR0"), float(C), Op.is_ge, -float(C), Op.mult),
-                    lambda: tt(W("t2"), W("LR0"), W("t1"), Op.add))
-            cp(U("OLC0"), W("t2"))
-            tt(W("dlp"), W("LR0"), W("par"), Op.subtract)
+        remote("S", rc, HALF)
         if rd == 0:
-            quant("e", "et", 0, 512)
+            fill(R("tl"), 0.0)
+            shift(R("pre"), R("zero"), 0.0, col("f1"))
+            act(R("pw0", 0, C), R("pre"))
+        ts(field("tl", COL), R(la, 0, K), -float(HALF), Op.add)
         if not last:
-            tt(R("lrf"), R("wa", 0, C), R("wa", 3 * C, 4 * C), Op.add)
+            act(R("ga", 0, C), R("tab2"), ll)
+        turn(R("tabp", 0, C), R("tl"))
+        turn(R("tabp", C, 2 * C), R("tl"))
+        cp(R("op", 0, 12), R(so, K + 11, K + 23))
+        m2 = unwrap(2, "tabp", R("op", 0, 11))
+        m2[0]()
+        if not last:
+            put(R("pw0"), ll, R("tab2", 0, C))
         else:
-            act(R("gro"), R("wa", 0, 2 * C), scale=2.0 ** 22)
-            store("y", T["gr"][:, :], T["gro"][0:128:16, :], R("gro"))
+            fill(R("grt"), 0.0)
             quant("v", "vt", 0, 128)
-        arrive("laM%d" % rd, "aM%d" % rd, 8)
-        own = R("laM%d" % rd, 0, 11)
-        for b in range(4):
+            cp(field("grt", 0), R("X", 32, 32 + K))
+            cp(field("grt", 1), R("X", 0, K))
+        for f in m2[1:]:
+            f()
+        if not last:
+            cp(R("ol", 0, K), ll)
+            turn(R("tpu"), R("pw0", 0, C))
+            turn(R("tga"), R("ga", 0, C))
+            name(0, "tpu", ID)
+        own = R("mo2", 0, 11)
+
+        def owns(b):
             x = R("xt", 4 * HALF + b, 4 * C, 4)
             tt(x, R("hp", C * b, C * b + C), x, Op.add, own)
+            if not last:
+                act(R("win", 704 * b + C + HALF, 704 * b + 2 * C), R("hp", C * b, C * b + C), own, scale=0.5)
+        owns(0)
+        if not last:
+            if rd == 0:
+                move(R("pw0", 0, C), R("pre"))
+            swap(1, lambda: owns(1))
+            owns(2)
+            cp(R("op"), R("X"), R("sel", 0, 2))
+        else:
+            owns(1)
+            owns(2)
+        owns(3)
         quant("x", "xt", HALF, C)
         if not last:
-            for b in range(4):
-                act(R("win", 704 * b + C + HALF, 704 * b + 2 * C), R("hp", C * b, C * b + C), own, scale=0.5)
+            mm(1, "ur", 0, "qx", "sx", HALF, C)
+            differences("t2")
+            tt(P("Z"), pair("tpu", RT), pair("t2", RT), Op.subtract)
+            tt(P("El"), pair("t2", RT), pair("t2", L), Op.subtract)
+            flags(1, HALF, C)
+            for t in range(4):
+                plane(t, HALF, C)
         else:
             mm(0, "v", 0, "qx", "sx", HALF, C)
+            turn(R("gro"), R("grt"))
             act(R("yo", HALF, C), R("ps0", 0, HALF))
             store("y", T["oc"][:, 4 * HALF:4 * C], T["qx"][:, HALF:C].bitcast(dt.uint8), R("qx", HALF, C))
             for k in range(4):
                 store("y", T["osc"][4 * k:4 * k + 4, HALF:C], T["sx"][32 * k:32 * k + 4, HALF:C], R("sx", HALF, C))
+            for k in range(2):
+                store("y", T["gr"][:, C * k:C * k + C], T["gro"][k:128:16, :], R("gro"))
             store("y", T["y"][:, HALF:C], T["yo"][:, HALF:C], R("yo", HALF, C))
+        if rd == 0:
+            quant("e", "et", 0, 512)
         arrive("laQ%d" % rd, "aC%d" % rd, 16)
         arrive("laS%d" % rd, "aS%d" % rd, 8)
         for b in range(4):
             mm(4 + b, "e", 128 * b, "laQ%d" % rd, "laS%d" % rd, 0, HALF)
-        if not last:
-            scores(HALF, C, 2)
         for b in range(4):
             x = R("xt", b, 4 * HALF, 4)
             tt(x, R("ps%d" % (4 + b), 0, HALF), x, Op.add)

@@ -6,11 +6,14 @@ Op, Act = AluOpType, ActivationFunctionType
 C, HALF, K = 352, 176, 22
 STEP = [1, 2, 4]
 CHUNKS = [(0, 192), (192, 352)]
-SENT = 34
+WAYS = 5
+THIRD = 60
+LW = 12
 L, RT, ID, COL = 0, 4, 1, 2
-PAIRS = ["act", "acd", "at", "dt", "Dl", "Db", "E", "El", "Z", "m1", "m2", "m3", "m4", "m5", "la", "ra", "rb"]
-INTS = [("p", 8), ("a", 8), ("b", 8), ("c", 8), ("d", 8), ("e", 8), ("j", 8), ("q", 8), ("n", 48), ("lo", 48), ("m", 24), ("lw", 24), ("rw", 24)]
-COLS = ["sig", "mb", "k", "h", "pm", "p32", "f1", "nf", "n2"]
+PAIRS = ["act", "acd", "at", "dt", "E", "El", "Z", "m4"]
+QUADS = ["D", "A", "M", "N"]
+INTS = [("p", 8), ("a", 8), ("b", 8), ("c", 8), ("d", 8), ("e", 8), ("f", 8), ("j", 8), ("q", 8), ("o", 4), ("n", 48), ("lo", 48), ("m", 24), ("lw", 24), ("rw", 24)]
+COLS = ["sig", "mb", "k", "h", "p32", "f1", "nf", "n2", "dn"]
 
 
 def codes_of(name, n):
@@ -22,54 +25,71 @@ def tiles(kind, **widths):
 
 
 SCRATCH = {
-    **tiles("bfloat16", xt=4 * C, lvt=4 * C, ut=512, vt=512, win=8 * C, gl=4 * C, zt=4 * C, hp=4 * C, gt=4 * HALF, et=2048, one=512,
-            sg=2 * C, ga=2 * C, gb=C, gp=C, pw0=2 * C, pw1=2 * C, pre=C, zero=C, town=C, tga=C, tgb=C, tpu=C, t2=C, tab2=2 * C, tl=C, tabp=2 * C,
-            g1=208, g2=208, mt1=384, mt2=384, dq=88, pr=48 * len(PAIRS)),
+    **tiles("bfloat16", xt=4 * C, lvt=4 * C, ut=512, vt=512, win=8 * C, gl=4 * C, zt=4 * C, hp=4 * C, gt=12 * THIRD, yo2=4 * HALF, et=2048, one=512,
+            sg=2 * C, ga=2 * C, gb=C, gp=C, pw0=2 * C, pw1=2 * C, pre=C, zero=512, town=C, tga=C, tgb=C, tpu=C, t2=C, tab2=2 * C, tl=C, tabp=2 * C,
+            g1=208, g2=224, mt1=736, mt2=736, dq=88, pr=48 * len(PAIRS), qd=96 * len(QUADS)),
     **codes_of("x", C), **codes_of("u", 128), **codes_of("ur", 128), **codes_of("v", 128), **codes_of("w", 512), **codes_of("e", 512), **codes_of("z", C),
     **{"i" + n: ("sbuf", [128, w], "int32") for n, w in INTS},
-    **tiles("uint16", ux=8, sel=4, ms=2, ol=32, op=32, mo1=16, mo2=16),
-    **tiles("float32", cols=24 * len(COLS), X=160, U=128, yo=C, grt=C, gro=C),
+    **tiles("uint16", ux=8, sel=4, ms=4, ol=32, op=32, mf=16, mo=16),
+    **tiles("float32", cols=24 * len(COLS), X=128, U=96, yo=C, grt=C, gro=C),
 }
 for _b in range(8):
     SCRATCH["ps%d" % _b] = ("psum", [128, 512], "float32")
 for _r in range(3):
     for _n in ("so", "ro", "la"):
-        SCRATCH["%sR%d" % (_n, _r)] = ("sbuf", [128, K + 48 if _n == "so" else SENT], "uint16")
-        SCRATCH["%sQ%d" % (_n, _r)] = ("sbuf", [128, HALF], "float8_e4m3fn_x4")
-        SCRATCH["%sS%d" % (_n, _r)] = ("sbuf", [128, HALF], "uint8")
-LOADS = ["lt", "rt", "x", "u", "lv", "wc", "ws", "v"]
-SEMAPHORES = (["cv", "cs", "ct", "cp", "ls", "outs"] + ["ld_" + n for n in LOADS] + ["d%d" % n for n in range(12)]
-              + ["a%s%d" % (n, r) for n in "RCS" for r in range(3)])
+        SCRATCH["%sR%d" % (_n, _r)] = ("sbuf", [128, 48 if _n == "so" else LW], "uint16")
+        SCRATCH["%sL%d" % (_n, _r)] = ("sbuf", [128, 24], "bfloat16")
+        SCRATCH["%sQ%d" % (_n, _r)] = ("sbuf", [128, 3 * THIRD + 128 if _n == "so" else 3 * THIRD], "float8_e4m3fn_x4")
+        SCRATCH["%sS%d" % (_n, _r)] = ("sbuf", [128, 3 * THIRD + 128 if _n == "so" else 4 * THIRD], "uint8")
+LOADS = ["lt", "rt", "x0", "x1", "u", "lv", "wc", "ws", "v"]
+SEMAPHORES = (["cv", "cs", "ct", "cp", "ls", "outs"] + ["ld_" + n for n in LOADS] + ["d%d" % n for n in range(20)]
+              + ["a%s%d" % (n, r) for n in "RLQS" for r in range(3)])
 
 
 def route(topo, core, partner):
     ok = [c for c in topo.cores_of(core) if c != core and topo.may_write(c, partner)]
-    near = [c for c in ok if topo.die(c) == topo.die(core)]
-    far = [c for c in ok if topo.die(c) != topo.die(core)]
-    return near[0], far[0], near[1]
+    return [c for c in ok if topo.die(c) == topo.die(core)] + [c for c in ok if topo.die(c) != topo.die(core)]
 
 
 def bits(engines):
     return sum(1 << e for e in engines)
 
 
+def pieces(rd, a, c, b, d):
+    every = list(range(16))
+    odd, even = every[1::2], every[0::2]
+    out = [("R", [("R", a, 0, LW, LW, every if rd else odd)])]
+    if WAYS == 5:
+        out += [("L", [("L", b, 0, 24, 24, every)] if rd else [("L", b, 0, 8, 8, even[:4]), ("L", c, 8, 16, 16, odd), ("L", d, 16, 24, 24, even[4:])]),
+                ("Q", [("Q", a, 0, 88, 88, odd), ("Q", b, 88, HALF, HALF, even)]), ("S", [("S", c, 0, 88, 88, odd), ("S", d, 88, HALF, HALF, even)])]
+    elif WAYS == 4:
+        out += [("L", [("L", b, 0, 24, 24, every)] if rd else [("L", b, 0, 8, 8, even[:4]), ("L", c, 8, 16, 16, odd), ("L", d, 16, 24, 24, even[4:])]),
+                ("Q", [("Q", a, 0, THIRD, THIRD, odd[:4]), ("Q", b, THIRD, 2 * THIRD, 2 * THIRD, even[:4]), ("Q", c, 2 * THIRD, 3 * THIRD, HALF, odd[4:]),
+                       ("S", d, 0, 4 * THIRD, HALF, even[4:])])]
+    else:
+        out += [("L", [("L", b, 0, 24, 24, every)] if rd else [("L", b, 0, 12, 12, even), ("L", c, 12, 24, 24, odd)]),
+                ("Q", [("Q", a, 0, 88, 88, odd), ("Q", b, 88, HALF, HALF, even)]), ("S", [("S", c, 0, HALF, HALF, every)])]
+    return out
+
+
+def view(T, name, lo, hi):
+    v = T[name][:, lo:hi]
+    return v.bitcast(dt.uint8) if name[2] == "Q" else v
+
+
 def relay_program(g, core, T, topo, rank):
     src, sent = T.cores[rank], 0
     for rd, s in enumerate(STEP):
         dst = T.cores[rank ^ s]
-        a, b, c = route(topo, src, dst)
-        if core not in (a, b, c):
-            continue
-        rid, pid = topo.addr(dst, core)
-        eng = topo.engines(core, dst)[:8]
-        jobs = {a: [("C", "Q", 0, 88, 8)], b: [("C", "Q", 88, HALF, 8)], c: [("R", "R", 0, SENT, 16), ("S", "S", 0, HALF, 16)]}[core]
-        for sem, buf, lo, hi, n in jobs:
-            g.wait_ge(T.sem["a%s%d" % (sem, rd)], n)
-            o, i = T["la%s%d" % (buf, rd)][:, lo:hi], T["ro%s%d" % (buf, rd)][:, lo:hi]
-            if buf == "Q":
-                o, i = o.bitcast(dt.uint8), i.bitcast(dt.uint8)
-            g.remote_dma(o, i, T.sem["a%s%d" % (sem, rd)], T.sem["ls"], pid, rid, bits(eng))
-            sent += len(eng)
+        for sem, parts in pieces(rd, *route(topo, src, dst)):
+            for buf, relay, lo, _, hi, on in parts:
+                if relay == core:
+                    rid, pid = topo.addr(dst, core)
+                    eng = topo.engines(core, dst)
+                    g.wait_ge(T.sem["a%s%d" % (sem, rd)], len(on))
+                    g.remote_dma(view(T, "la%s%d" % (buf, rd), lo, hi), view(T, "ro%s%d" % (buf, rd), lo, hi), T.sem["a%s%d" % (sem, rd)], T.sem["ls"],
+                                 pid, rid, bits(eng))
+                    sent += len(eng)
     if sent:
         g.wait_ge(T.sem["ls"], sent)
 
@@ -154,11 +174,21 @@ def rank_program(g, core, T, topo):
     def P(name):
         return R("pr", 48 * PAIRS.index(name), 48 * PAIRS.index(name) + 2 * K)
 
+    def Q(name, side=None):
+        at = 96 * QUADS.index(name)
+        return R("qd", at, at + 4 * K) if side is None else R("qd", at + side, at + 4 * K, 2)
+
+    def quad(name):
+        return (name, 0, C, 4)
+
     def pair(name, f):
         return (name, f, C, 8)
 
     def field(name, f):
         return (name, f, C, 16)
+
+    def part(r, lo, hi):
+        return (r[0], r[1] + lo // 16, r[1] + hi // 16, 1)
 
     def ap(r):
         return T[r[0]][:, r[1]:r[2]] if r[3] == 1 else T[r[0]][:, r[1]:r[2]:r[3]]
@@ -202,42 +232,41 @@ def rank_program(g, core, T, topo):
     def shift(out, in_, scale, bias):
         run("s", lambda: g.scalar.activation(ap(out), ap(in_), Act.Identity, bias=num(bias), scale=scale), given(in_, bias), [out])
 
-    def quant(name, tile, lo, hi, q=None, s=None):
-        q, s = q or "q" + name, s or "s" + name
+    def quant(name, tile, lo, hi, q=None, s=None, at=None):
+        q, s, at = q or "q" + name, s or "s" + name, lo if at is None else at
         t = R(tile, 4 * lo, 4 * hi)
-        run("v", lambda: g.vector.quantize_mx(T[q][:, lo:hi], T[s][:, lo:hi], ap(t)), [t], [R(q, lo, hi), R(s, lo, hi)])
+        run("v", lambda: g.vector.quantize_mx(T[q][:, at:at + hi - lo], T[s][:, at:at + hi - lo], ap(t)), [t], [R(q, at, at + hi - lo), R(s, at, at + hi - lo)])
 
     def mm(bank, w, wlo, q, s, lo, hi):
         p, wq, wsc = "ps%d" % bank, "q" + w, "s" + w
         run("t", lambda: g.tensor.matmul_mx(T[p][:, 0:hi - lo], T[wq][:, wlo:wlo + 128], T[wsc][:, wlo:wlo + 128], T[q][:, lo:hi], T[s][:, lo:hi], True, True),
             [R(wq, wlo, wlo + 128), R(wsc, wlo, wlo + 128), R(q, lo, hi), R(s, lo, hi)], [R(p)])
 
-    def arrive(name, sem, n):
-        note("p", (sem, n), [], [R(name)])
+    def arrive(reg, sem, n):
+        note("p", (sem, n), [], [reg])
         clocks[(sem, n)] = {}
-
-    def send(rds, fn, n):
-        before("p", rds, [])
-        fn()
-        count["ls"] += n
 
     def iota(out, pattern, base, cm):
         run("p", lambda: g.iota(ap(out), pattern, base, cm), [], [out])
 
-    def swap(n, *between):
-        for k in range(2 * n):
-            turn(R("U", 32 * k, 32 * k + 32), R("X", 32 * (k // 2), 32 * (k // 2) + 32))
-        for f in between:
-            f()
-        turn(R("X", 64, 64 * n + 32), R("U", 16, 64 * n - 16))
+    def swap(first=None, then=None):
+        turn(R("U", 0, 64), R("X", 0, 64))
+        turn(R("U", 64, 96), R("X", 0, 32))
+        if first:
+            first()
+        turn(R("X", 64, 128), R("U", 16, 80))
+        if then:
+            then()
 
     def name(k, buf, f):
         tt(R("X", 32 * k, 32 * k + K), field(buf, f), field(buf, f + 8), Op.add)
 
-    load("y", "ld_lt", T["ilw"][:, 0:K], T["lt"][:], I("lw"))
-    load("s", "ld_rt", T["irw"][:, 0:K], T["rt"][:], I("rw"))
     load("y", "ld_u", T["ut"][:], T["u"][:], R("ut"))
-    load("s", "ld_x", T["xt"][:], T["x"][:], R("xt"))
+    load("s", "ld_lt", T["ilw"][:, 0:K], T["lt"][:], I("lw"))
+    load("s", "ld_rt", T["irw"][:, 0:K], T["rt"][:], I("rw"))
+    for h in range(2):
+        load("ys"[h], "ld_x%d" % h, T["xt"][:, 704 * h:704 * h + 704], T["x"][:, 704 * h:704 * h + 704], R("xt", 704 * h, 704 * h + 704))
+    before("y", [R("xt")], [])
     load("y", "ld_lv", T["lvt"][:], T["lv"][:], R("lvt"))
     load("y", "ld_wc", T["qw"][:, 0:512].bitcast(dt.uint8), T["wc"][:, 0:2048], R("qw"))
     load("y", "ld_ws", T["sw"][:, 0:512], T["ws"][:, 0:512], R("sw"))
@@ -246,290 +275,287 @@ def rank_program(g, core, T, topo):
     iota(I("p"), [[0, 8]], 0, 1)
     iota(I("j"), [[16, 8]], 0, 0)
     iota(I("m", 0, K), [[32, 11], [0, 2]], 0, 0)
-    fill(R("X"), 0.0)
+    iota(I("o"), [[11, 2], [0, 2]], 0, 0)
     fill(R("zero"), 0.0)
-    fill(R("one"), 1.0)
-    ts(I("a"), I("p"), 15, Op.bitwise_and)
-    ts(I("b"), I("p"), 4, Op.arith_shift_right, 1, Op.bitwise_and)
+    shift(R("one"), R("zero"), 0.0, 1.0)
+    act(R("X"), R("zero", 0, 128))
     ts(I("c"), I("p"), 3, Op.bitwise_and)
     ts(I("d"), I("p"), 1, Op.arith_shift_right, 2, Op.bitwise_and)
-    ts(I("e"), I("p"), 31, Op.bitwise_and)
-    tt(I("q"), I("a"), I("j"), Op.add)
-    cp(col("h"), I("b", 0, 1))
+    ts(I("a"), I("p"), 15, Op.bitwise_and)
+    ts(I("b"), I("p"), 4, Op.arith_shift_right, 1, Op.bitwise_and)
     ts(col("mb"), I("c", 0, 1), 3.0, Op.is_equal)
     ts(col("nf"), I("c", 0, 1), 2.0, Op.is_equal, -2.0, Op.mult)
     ts(col("n2"), I("c", 0, 1), 0.0, Op.is_gt)
-    ts(col("f1"), I("a", 0, 1), float(ID), Op.is_equal, float(C), Op.mult)
-    cp(col("p32"), I("e", 0, 1))
-    ts(I("e"), I("q"), float(K), Op.is_ge)
+    tt(I("q"), I("a"), I("j"), Op.add)
     tt(col("k"), col("mb"), I("d", 0, 1), Op.add)
+    cp(col("h"), I("b", 0, 1))
+    ts(I("e"), I("q"), float(K), Op.is_ge)
     tt(col("sig"), col("nf"), col("n2"), Op.add)
-    ts(I("c"), I("e"), -float(K), Op.mult)
     ts(R("ux"), I("j"), col("k"), Op.add)
-    tt(I("q"), I("q"), I("c"), Op.add)
+    ts(I("c"), I("e"), -float(K), Op.mult)
     ts(I("d"), I("e"), 32.0, Op.mult, col("h"), Op.add)
-    ts(I("e"), I("e"), 32.0, Op.mult, 64.0, Op.add)
+    ts(I("b"), I("e"), -64.0, Op.mult, 32.0, Op.add)
+    tt(I("q"), I("q"), I("c"), Op.add)
+    ts(I("f"), I("p"), 31, Op.bitwise_and)
+    ts(I("b"), I("b"), col("h"), Op.mult, 64.0, Op.add)
     ts(I("c"), I("q"), 1, Op.bitwise_and)
-    ts(I("q"), I("q"), 62, Op.bitwise_and)
+    ts(I("e"), I("q"), 62, Op.bitwise_and)
+    ts(col("f1"), I("a", 0, 1), float(ID), Op.is_equal, float(C), Op.mult)
     ts(I("c"), I("c"), col("h"), Op.not_equal)
-    tt(I("q"), I("q"), I("d"), Op.add)
-    tt(I("c"), I("c"), I("e"), Op.mult)
+    tt(I("q"), I("e"), I("d"), Op.add)
+    cp(col("p32"), I("f", 0, 1))
+    tt(I("c"), I("c"), I("b"), Op.mult)
+    act(R("pw0", 0, C), R("zero", 0, C))
+    act(R("ga", C, 2 * C), R("zero", 0, C))
+    act(R("t2"), R("zero", 0, C))
     quant("u", "ut", 0, 128)
     tt(I("q"), I("q"), I("c"), Op.add)
-    cp(R("X", 0, K), I("rw", 0, K))
-    cp(R("X", 32, 32 + K), I("lw", 0, K))
+    run("v", lambda: g.vector.tensor_copy(T["qur"][:].bitcast(dt.uint32), T["qu"][:].bitcast(dt.uint32).indirect(T["ux"][:])), [R("qu"), R("ux")], [R("qur")])
+    run("s", lambda: g.scalar.activation(T["sur"][:], T["su"][:].indirect(T["ux"][:]), Act.Copy), [R("su"), R("ux")], [R("sur")])
     cp(R("sel"), I("q", 0, 4))
-
-    def replicas():
-        run("v", lambda: g.vector.tensor_copy(T["qur"][:].bitcast(dt.uint32), T["qu"][:].bitcast(dt.uint32).indirect(T["ux"][:])),
-            [R("qu"), R("ux")], [R("qur")])
-        run("s", lambda: g.scalar.activation(T["sur"][:], T["su"][:].indirect(T["ux"][:]), Act.Copy), [R("su"), R("ux")], [R("sur")])
-
-    swap(2, replicas)
-    cp(R("ol", 0, K), I("lw", 0, K))
-    cp(I("n"), R("X"), R("sel", 0, 3))
-    quant("x", "xt", 0, C)
-    ts(I("lo"), I("n"), 31, Op.bitwise_and)
-    act(R("pw0", 0, C), R("zero"))
-    act(R("ga", C, 2 * C), R("zero"))
-    mm(0, "ur", 0, "qx", "sx", 0, C)
-    for f, at in ((0, K), (1, 0)):
-        tt(R("dq", f, 88, 4), I("n", at, at + K), I("lo", at, at + K), Op.subtract)
-        cp(R("dq", 2 + f, 88, 4), I("lo", at, at + K))
     for b in range(4):
         run("p", lambda: g.affine_select(T["et"][:, 512 * b:512 * b + 512], T["one"][:], [[-1, 512]], Op.is_equal, 0.0, b, 4),
             [R("one")], [R("et", 512 * b, 512 * b + 512)])
 
+    def scores(bank, lo, hi):
+        for k in range(2):
+            mm(bank + k, "ur", 0, "qx", "sx", lo, hi)
+        act(R("sg", C + lo, C + hi), R("ps%d" % (bank + 1), 0, hi - lo), func=Act.Sign, scale=col("mb"))
+
     def flags(bank, lo, hi):
         ts(R("sg", lo, hi), R("ps%d" % bank, 0, hi - lo), col("sig"), Op.mult, 0.0, Op.is_gt)
-        act(R("sg", C + lo, C + hi), R("ps%d" % bank, 0, hi - lo), func=Act.Sign, scale=col("mb"))
 
-    def plane(t, lo, hi):
-        act(R("win", 704 * t + lo, 704 * t + hi), R("xt", 4 * lo + t, 4 * hi, 4), scale=0.5)
+    cp(R("X", 0, K), I("rw", 0, K))
+    cp(R("X", 32, 32 + K), I("lw", 0, K))
+    quant("x", "xt", 0, HALF)
+    scores(0, 0, HALF)
+    swap(lambda: cp(R("ol", 0, K), I("lw", 0, K)), lambda: flags(0, 0, HALF))
+    cp(I("n"), R("X"), R("sel", 0, 3))
+    quant("x", "xt", HALF, C)
+    scores(2, HALF, C)
+    ts(I("lo"), I("n"), 31, Op.bitwise_and)
+    tt(I("o"), I("o"), I("a", 0, 4), Op.add)
+    for f, at in ((0, K), (1, 0)):
+        tt(R("dq", f, 88, 4), I("n", at, at + K), I("lo", at, at + K), Op.subtract)
+        cp(R("dq", f + 2, 88, 4), I("lo", at, at + K))
+    flags(2, HALF, C)
+    ts(I("c", 0, 4), I("o"), col("h"), Op.add)
+    turn(R("town"), R("sg", 0, C))
+    cp(field("t2", ID), I("m", 0, K))
+    cp(quad("town"), R("dq"))
+    ts(field("t2", ID + 8), R("zero", 0, K), col("p32"), Op.add)
+    turn(R("sg", 0, C), R("town"))
+
+    def plane(t):
+        act(R("win", 704 * t, 704 * t + C), R("xt", t, 4 * C, 4), scale=0.5)
 
     def differences(own):
         l, r = pair(own, L), pair(own, RT)
-        tt(P("Dl"), pair("tga", L), l, Op.subtract)
-        tt(P("Db"), pair("tga", RT), r, Op.subtract)
-        tt(P("E"), l, pair("tga", RT), Op.subtract)
+        return [lambda: tt(Q("D"), quad("tga"), quad(own), Op.subtract), lambda: tt(P("E"), l, pair("tga", RT), Op.subtract),
+                lambda: tt(P("Z"), pair("tpu", RT), r, Op.subtract), lambda: tt(P("El"), r, l, Op.subtract)]
 
-    def step(j, own, out, ready, pw, gap):
-        l, r = pair(own, L), pair(own, RT)
-        ol = R("ol", 0, K)
+    def step(j, own, out, ol, ready, pw, gap):
         pos, neg, way = 1 + 4 * j, 2 + 4 * j, 3 + 4 * j
         act(R("ga", 0, C), R("sg"), ol, func=Act.Relu)
         act(R("gb"), R("ga"), ol)
         gap()
+        d = differences(own)
         if ready:
             cp(R("gp"), R("sg"), R("op", 0, K))
-            turn(R("town"), R("sg", 0, C))
             turn(R("tga"), R("ga", 0, C))
             turn(R("tpu"), R("gp"))
         else:
-            tt(P("El"), r, l, Op.subtract)
             put(R(pw), ol, R("sg", 0, C))
             turn(R("tga"), R("ga", 0, C))
             turn(R("tpu"), R(pw, 0, C))
             turn(R("tgb"), R("gb"))
-            differences(own)
-            tt(P("Z"), pair("tpu", RT), r, Op.subtract)
+            d[0]()
         tt(P("act"), pair("town", pos), pair("tga", neg), Op.mult)
         tt(P("acd"), pair("town", neg), pair("tpu", pos), Op.mult)
         late = lambda: tt(P("at"), P("act"), pair("tgb", way), Op.mult)
         if not ready:
+            d[2](), d[1]()
             late()
-        tt(P("m5"), P("act"), P("Db"), Op.mult)
+        tt(Q("M", 1), P("act"), Q("D", 1), Op.mult)
         tt(P("dt"), P("acd"), pair("tga", way), Op.mult)
         tt(P("m4"), P("acd"), P("Z"), Op.mult)
         if ready:
+            tt(Q("M", 0), P("dt"), P("El"), Op.mult)
             turn(R("tgb"), R("gb"))
-        tt(P("ra"), r, P("m5"), Op.add)
-        tt(P("m2"), P("dt"), P("El"), Op.mult)
-        if ready:
+            tt(Q("A"), quad(own), Q("M"), Op.add)
             late()
-        tt(P("rb"), P("ra"), P("m4"), Op.add)
-        tt(P("la"), l, P("m2"), Op.add)
-        tt(P("m1"), P("at"), P("Dl"), Op.mult)
-        tt(P("m3"), P("at"), P("E"), Op.mult)
-        tt(pair(out, L), P("la"), P("m1"), Op.add)
-        tt(pair(out, RT), P("rb"), P("m3"), Op.add)
+            a, at = Q("A"), P("at")
+            tt(col("n2", K), (a[0], a[1], a[2], 4), (a[0], a[1] + 2, a[2], 4), Op.add)
+            tt(col("nf", K), (at[0], at[1], at[2], 2), col("dn", K), Op.mult)
+            tt(Q("N", 0), at, Q("D", 0), Op.mult)
+            tt(R("X", 0, K), col("n2", K), col("nf", K), Op.add)
+            tt(Q("N", 1), at, P("E"), Op.mult)
+            tt(Q("A", 1), Q("A", 1), P("m4"), Op.add)
+            swap(lambda: tt(quad(out), a, Q("N"), Op.add), lambda: turn(R("sg", 0, C), R(out)))
+            return
+        tt(Q("N", 0), P("at"), Q("D", 0), Op.mult)
+        if not ready:
+            tt(Q("M", 0), P("dt"), P("El"), Op.mult)
+        tt(Q("N", 1), P("at"), P("E"), Op.mult)
+        if not ready:
+            tt(Q("A"), quad(own), Q("M"), Op.add)
+            tt(Q("N", 1), Q("N", 1), P("m4"), Op.add)
+        tt(quad(out), Q("A"), Q("N"), Op.add)
 
-    def unwrap(k, tab, lst):
-        gk, mt = "g%d" % k, "mt%d" % k
-        return [lambda: act(R(gk, 16, 192), R(tab), lst),
-                lambda: turn(R(mt, 0, 192), R(gk, 16, 208)), lambda: turn(R(mt, 192, 384), R(gk, 0, 192)),
-                lambda: ts(R("mo%d" % k, 0, 16), R(mt), float(HALF), Op.add, ind=R("ms", 0, 1))]
-
+    differences("town")[3]()
+    ll = R("ol", 0, K)
     for rd in range(3):
         last = rd == 2
         partner = T.cores[rank ^ STEP[rd]]
-        ra, rb, rc = route(topo, core, partner)
-        so, la = "soR%d" % rd, "laR%d" % rd
+        plan = pieces(rd, *route(topo, core, partner))
+        q, s, lists = "soQ%d" % rd, "soS%d" % rd, "soR%d" % rd
 
-        def to(relay, lo, n):
-            return bits(topo.engines(core, relay)[lo:lo + n])
-
-        def remote(buf, relay, n):
-            rid, pid = topo.addr(relay, core)
-            o, i = T["ro%s%d" % (buf, rd)], T["so%s%d" % (buf, rd)]
-            send([R("so%s%d" % (buf, rd), 0, n)],
-                 lambda: g.remote_dma(o[:], i[:, 0:n], T.sem["a%s%d" % (buf, rd)], T.sem["ls"], pid, rid, to(relay, 0, 16)), 16)
-
-        if rd == 0:
-            flags(0, 0, C)
-            turn(R("town"), R("sg", 0, C))
-            ts(I("c"), I("a"), col("h"), Op.add)
-            cp(R("town", 0, C, 4), R("dq"))
-            ts(I("d"), I("a"), 16.0, Op.mult, float(COL), Op.add)
-            turn(R("sg", 0, C), R("town"))
-            ts(I("c"), I("c"), 1, Op.bitwise_and)
-        else:
-            mm(0, "ur", 0, "qx", "sx", 0, HALF)
-            flags(0, 0, HALF)
+        def remote(k):
+            sem, parts = plan[k]
+            before("p", [R("so%s%d" % (buf, rd), lo, hi) for buf, _, lo, hi, _, _ in parts], [])
+            tr, total = [], sum(len(topo.engines(p[1], partner)) for p in parts)
+            for buf, relay, lo, hi, end, on in parts:
+                rid, pid = topo.addr(relay, core)
+                tr.append(RemoteDMATransfer(dst_ids=[DstId(rid=rid, pnc=pid)], dma_engine_mask=bits(topo.engines(core, relay)[e] for e in on),
+                                            remote_sem=T.sem["a%s%d" % (sem, rd)],
+                                            src=view(T, "so%s%d" % (buf, rd), lo, hi), dst=view(T, "ro%s%d" % (buf, rd), lo, hi)))
+                arrive(R("la%s%d" % (buf, rd), lo, end), "a%s%d" % (sem, rd), total)
+            g.remote_dma_fused(tr, local_sem=T.sem["ls"])
+            count["ls"] += sum(len(p[5]) for p in parts)
 
         def gap0():
             if rd == 0:
-                act(R("pw1", 0, C), R("zero"))
-                for t in range(3):
-                    plane(t, 0, C)
-            else:
-                for t in range(4):
-                    act(R("win", 704 * t + C, 704 * t + C + HALF), R("ps%d" % (4 + t), 0, HALF), scale=0.5)
-                for t in range(2):
-                    plane(t, 0, HALF)
+                act(R("pw1", 0, C), R("zero", 0, C))
+            for t in range(4):
+                plane(t)
 
         def gap1():
-            if rd == 0:
-                plane(3, 0, C)
-                for t in range(4):
+            for t in range(4):
+                if rd == 0:
                     act(R("win", 704 * t + C, 704 * t + 2 * C), R("lvt", t, 4 * C, 4), scale=0.5)
-            else:
-                for t in range(2, 4):
-                    plane(t, 0, HALF)
+                else:
+                    act(R("win", 704 * t + C, 704 * t + C + HALF), R("ps%d" % (4 + t), 0, HALF), scale=0.5)
+                    act(R("win", 704 * t + C + HALF, 704 * t + 2 * C), R("yo2", HALF * t, HALF * t + HALF), scale=0.5)
+            if rd == 0:
+                shift(R("pre"), R("zero", 0, C), 0.0, col("f1"))
+                for o in (R("g1"), R("gt", 4 * HALF, 12 * THIRD), R("mt1", 192, C), R("mt1", 544, 736), R("tl"), R("g2", 192, 224), R("mt2", C, 544)):
+                    move(o, R("zero", 0, o[2] - o[1]))
 
-        step(0, "town" if rd == 0 else "t2", "town", rd > 0, "pw0", gap0)
-        name(0, "town", L)
-        swap(1, lambda: turn(R("sg", 0, C), R("town")))
+        step(0, "town" if rd == 0 else "t2", "town", ll, rd > 0, "pw0", gap0)
         if rd == 0:
-            fill(R("t2"), 0.0)
+            ts(I("c", 0, 4), I("c", 0, 4), 1, Op.bitwise_and)
+            name(0, "town", L)
+            ts(I("o"), I("o"), 16.0, Op.mult, float(COL), Op.add)
+            swap(lambda: turn(R("sg", 0, C), R("town")), lambda: ts(I("c", 0, 4), I("c", 0, 4), C + 16.0, Op.mult))
         cp(R("ol"), R("X"), R("sel", 0, 2))
-        if rd == 0:
-            ts(I("c"), I("c"), 208.0, Op.mult)
-            cp(field("t2", ID), I("m", 0, K))
-            ts(field("t2", ID + 8), R("zero", 0, K), col("p32"), Op.add)
-            tt(I("c"), I("c"), I("d"), Op.add)
-            ts(R("ms"), I("c", 0, 2), 383.0, Op.min)
-        step(1, "town", "t2", False, "pw1", gap1)
+        differences("town")[3]()
+        step(1, "town", "t2", R("ol", 0, K), False, "pw1", gap1)
+        fill(R("soL%d" % rd, K, 24), 0.0)
         name(0, "t2", RT)
         name(1, "t2", L)
         nl = R("X", 32, 32 + K)
-        swap(2, lambda: ts(col("nf", K), nl, float(C), Op.is_ge, -float(C), Op.mult))
-        tt(col("n2", K), nl, col("nf", K), Op.add)
-        cp(R(so, K, K + 48), R("X"), R("sel", 0, 3))
-        cp(R(so, 0, K), col("n2", K))
-        remote("R", rc, SENT)
-        ts(field("t2", COL), col("n2", K), -float(HALF), Op.add)
-        lr, ll = R(so, K, 2 * K), R(so, 2 * K, 3 * K)
-        part = lambda r, lo, hi: (r[0], r[1] + lo // 16, r[1] + hi // 16, 1)
+        swap(lambda: ts(col("nf", K), nl, float(C), Op.is_ge, -float(C), Op.mult), lambda: ts(col("n2", K), nl, -float(HALF), Op.add))
+        cp(R(lists), R("X"), R("sel", 0, 3))
+        remote(0)
+        tt(field("t2", COL), col("n2", K), col("nf", K), Op.add)
+        tt(R("soL%d" % rd, 0, K), col("n2", K), col("nf", K), Op.add)
+        remote(1)
         turn(R("tab2", 0, C), R("t2"))
         move(R("tab2", C, 2 * C), R("tab2", 0, C))
+        if WAYS == 4:
+            quant("", "zero", 0, 128, q, s, 3 * THIRD)
         if not last:
-            move(R("pw1", 0, C), R("zero"))
+            move(R("pw1", 0, C), R("zero", 0, C))
+        if rd == 0:
+            move(R("pw0", 0, C), R("pre"))
+            tt(I("c", 0, 4), I("c", 0, 4), I("o"), Op.add)
+        lr, ll = R(lists, 0, K), R(lists, K, 2 * K)
+
+        def layer(h, b, on):
+            lo, hi = CHUNKS[h]
+            o, i = R("hp", C * b + lo, C * b + hi), R("ps%d" % (4 * h + b), 0, hi - lo)
+            if on == "v":
+                ts(o, i, 0.03125, Op.mult)
+            else:
+                act(o, i, scale=0.03125)
+
         for h, (lo, hi) in enumerate(CHUNKS):
             for t in range(4):
                 act(R("gl", C * t + lo, C * t + hi), R("win", 704 * t, 704 * t + 704), part(ll, lo, hi))
+            for t in range(4 * h):
+                layer(0, t, "s")
+            for t in range(4):
                 tt(R("zt", 4 * lo + t, 4 * hi, 4), R("win", 704 * t, 704 * t + 704), R("gl", C * t + lo, C * t + hi), Op.add, part(lr, lo, hi))
             quant("z", "zt", lo, hi)
             for b in range(4):
                 mm(4 * h + b, "w", 128 * b, "qz", "sz", lo, hi)
+        act(R("g1", 16, 192), R("tab2"), R("laR%d" % rd, 0, 11))
+        push = [lambda lo=lo, hi=hi: put(R("pw0"), part(ll, lo, hi), R("tab2", lo, hi)) for lo, hi in CHUNKS]
+        wanted = [lambda: turn(R("mt1", 0, 192), R("g1", 16, 208)), lambda: turn(R("mt1", C, C + 192), R("g1", 0, 192)),
+                  lambda: ts(R("mf"), R("mt1"), float(HALF), Op.add, ind=R("ms", 0, 1))]
         if rd == 0:
-            fill(R("g1"), 0.0)
-            fill(R("g2"), 0.0)
-        arrive(la, "aR%d" % rd, 8)
-        m1 = unwrap(1, "tab2", R(la, K, K + 11))
-        for h, (lo, hi) in enumerate(CHUNKS):
-            if h == 1:
-                m1[0]()
+            ts(R("ms"), I("c", 0, 4), 735.0, Op.min)
+            quant("e", "et", 0, 512)
             for b in range(4):
-                o, i = R("hp", C * b + lo, C * b + hi), R("ps%d" % (4 * h + b), 0, hi - lo)
-                if h == 1 and b < 3:
-                    ts(o, i, 0.03125, Op.mult)
-                else:
-                    act(o, i, scale=0.03125)
-        for f in m1[1:]:
-            f()
+                layer(1, b, "v")
+            push[0]()
+            wanted[0](), wanted[1](), wanted[2]()
+        else:
+            wanted[0](), wanted[1]()
+            layer(1, 0, "v"), layer(1, 1, "s")
+            wanted[2]()
+            layer(1, 2, "v"), layer(1, 3, "s")
         for b in range(4):
-            o, i, n = R("gt", b, 4 * HALF, 4), R("hp", C * b, C * b + C), R("mo1", 0, 11)
-            if b % 2 == 0:
-                cp(o, i, n)
-            else:
-                act(o, i, n)
-        q, s = "soQ%d" % rd, "soS%d" % rd
-        quant("", "gt", 0, HALF, q, s)
-
-        def codes():
-            tr = []
-            for relay, lo, e in ((ra, 0, 0), (rb, 88, 8)):
-                rid, pid = topo.addr(relay, core)
-                tr.append(RemoteDMATransfer(dst_ids=[DstId(rid=rid, pnc=pid)], dma_engine_mask=to(relay, e, 8), remote_sem=T.sem["aC%d" % rd],
-                                            src=T[q][:, lo:lo + 88].bitcast(dt.uint8), dst=T["roQ%d" % rd][:, lo:lo + 88].bitcast(dt.uint8)))
-            g.remote_dma_fused(tr, local_sem=T.sem["ls"])
-        send([R(q)], codes, 16)
-        remote("S", rc, HALF)
-        if rd == 0:
-            fill(R("tl"), 0.0)
-            shift(R("pre"), R("zero"), 0.0, col("f1"))
-            act(R("pw0", 0, C), R("pre"))
-        ts(field("tl", COL), R(la, 0, K), -float(HALF), Op.add)
+            (act if b % 2 else cp)(R("gt", b, 4 * HALF, 4), R("hp", C * b, C * b + C), R("mf", 0, 11))
+        quant("", "gt", 0, 3 * THIRD if WAYS == 4 else HALF, q, s)
+        for k in range(2, len(plan)):
+            remote(k)
         if not last:
             act(R("ga", 0, C), R("tab2"), ll)
+        cp(field("tl", COL), R("laL%d" % rd, 0, K))
         turn(R("tabp", 0, C), R("tl"))
         turn(R("tabp", C, 2 * C), R("tl"))
-        cp(R("op", 0, 12), R(so, K + 11, K + 23))
-        m2 = unwrap(2, "tabp", R("op", 0, 11))
-        m2[0]()
-        if not last:
-            put(R("pw0"), ll, R("tab2", 0, C))
-        else:
+        act(R("g2", 0, 192), R("tabp"), part(lr, 160, C))
+        if rd == 1:
+            push[0]()
+        if last:
             fill(R("grt"), 0.0)
             quant("v", "vt", 0, 128)
             cp(field("grt", 0), R("X", 32, 32 + K))
             cp(field("grt", 1), R("X", 0, K))
-        for f in m2[1:]:
-            f()
+        turn(R("mt2", 160, C), R("g2", 0, 192))
+        turn(R("mt2", C + 192, 736), R("g2", 16, 208))
         if not last:
-            cp(R("ol", 0, K), ll)
-            turn(R("tpu"), R("pw0", 0, C))
             turn(R("tga"), R("ga", 0, C))
-            name(0, "tpu", ID)
-        own = R("mo2", 0, 11)
+        ts(R("mo"), R("mt2"), float(HALF), Op.add, ind=R("ms", 2, 3))
+        own = R("mo", 0, 11)
+        for b in range(4):
+            if not last or b % 2:
+                act(R("yo2", HALF * b, HALF * b + HALF), R("hp", C * b, C * b + C), own)
 
         def owns(b):
             x = R("xt", 4 * HALF + b, 4 * C, 4)
-            tt(x, R("hp", C * b, C * b + C), x, Op.add, own)
-            if not last:
-                act(R("win", 704 * b + C + HALF, 704 * b + 2 * C), R("hp", C * b, C * b + C), own, scale=0.5)
-        owns(0)
+            if not last or b % 2:
+                tt(x, R("yo2", HALF * b, HALF * b + HALF), x, Op.add)
+            else:
+                tt(x, R("hp", C * b, C * b + C), x, Op.add, own)
         if not last:
+            push[1]()
+            owns(0)
+            turn(R("tpu"), R("pw0", 0, C))
+            owns(1)
+            name(0, "tpu", ID)
+            owns(2)
             if rd == 0:
                 move(R("pw0", 0, C), R("pre"))
-            swap(1, lambda: owns(1))
-            owns(2)
+            swap(lambda: owns(3))
+            quant("x", "xt", HALF, C)
+            scores(0, HALF, C)
             cp(R("op"), R("X"), R("sel", 0, 2))
+            flags(0, HALF, C)
         else:
-            owns(1)
-            owns(2)
-        owns(3)
-        quant("x", "xt", HALF, C)
-        if not last:
-            mm(1, "ur", 0, "qx", "sx", HALF, C)
-            differences("t2")
-            tt(P("Z"), pair("tpu", RT), pair("t2", RT), Op.subtract)
-            tt(P("El"), pair("t2", RT), pair("t2", L), Op.subtract)
-            flags(1, HALF, C)
-            for t in range(4):
-                plane(t, HALF, C)
-        else:
+            owns(0), owns(2), owns(1), owns(3)
+            quant("x", "xt", HALF, C)
             mm(0, "v", 0, "qx", "sx", HALF, C)
             turn(R("gro"), R("grt"))
             act(R("yo", HALF, C), R("ps0", 0, HALF))
@@ -539,21 +565,25 @@ def rank_program(g, core, T, topo):
             for k in range(2):
                 store("y", T["gr"][:, C * k:C * k + C], T["gro"][k:128:16, :], R("gro"))
             store("y", T["y"][:, HALF:C], T["yo"][:, HALF:C], R("yo", HALF, C))
-        if rd == 0:
-            quant("e", "et", 0, 512)
-        arrive("laQ%d" % rd, "aC%d" % rd, 16)
-        arrive("laS%d" % rd, "aS%d" % rd, 8)
         for b in range(4):
             mm(4 + b, "e", 128 * b, "laQ%d" % rd, "laS%d" % rd, 0, HALF)
         for b in range(4):
             x = R("xt", b, 4 * HALF, 4)
             tt(x, R("ps%d" % (4 + b), 0, HALF), x, Op.add)
         quant("x", "xt", 0, HALF)
+        if not last:
+            scores(2, 0, HALF)
+            for f in differences("t2"):
+                f()
+            d = Q("D")
+            tt(col("dn", K), (d[0], d[1], d[2], 4), (d[0], d[1] + 2, d[2], 4), Op.add)
+            flags(2, 0, HALF)
+            turn(R("town"), R("sg", 0, C))
     mm(1, "v", 0, "qx", "sx", 0, HALF)
-    act(R("yo", 0, HALF), R("ps1", 0, HALF))
     store("y", T["oc"][:, 0:4 * HALF], T["qx"][:, 0:HALF].bitcast(dt.uint8), R("qx", 0, HALF))
     for k in range(4):
-        store("s" if k % 2 else "y", T["osc"][4 * k:4 * k + 4, 0:HALF], T["sx"][32 * k:32 * k + 4, 0:HALF], R("sx", 0, HALF))
+        store("s" if k == 0 else "y", T["osc"][4 * k:4 * k + 4, 0:HALF], T["sx"][32 * k:32 * k + 4, 0:HALF], R("sx", 0, HALF))
+    cp(R("yo", 0, HALF), R("ps1", 0, HALF))
     store("s", T["y"][:, 0:HALF], T["yo"][:, 0:HALF], R("yo", 0, HALF))
     for s in sorted(count):
         g.wait_ge(T.sem[s], count[s])

import math
from concourse.bass import DstId, RemoteDMATransfer
from concourse.mybir import dt, AluOpType, ActivationFunctionType

Op, Act = AluOpType, ActivationFunctionType
C, HALF, K = 352, 176, 22
STEP = [1, 2, 4]
CHUNKS = [(0, 192), (192, 352)]
WAYS = 5
THIRD = 60
LW = 12
L, RT, ID, COL = 0, 4, 1, 2
PAIRS = ["act", "acd", "at", "dt", "E", "El", "Z", "m4"]
QUADS = ["D", "A", "M", "N"]
INTS = [("p", 8), ("a", 8), ("b", 8), ("c", 8), ("d", 8), ("e", 8), ("f", 8), ("j", 8), ("q", 8), ("o", 4), ("n", 48), ("lo", 48), ("m", 24), ("lw", 24), ("rw", 24)]
COLS = ["sig", "mb", "k", "h", "p32", "f1", "nf", "n2", "dn"]


def codes_of(name, n):
    return {"q" + name: ("sbuf", [128, n], "float8_e4m3fn_x4"), "s" + name: ("sbuf", [128, n], "uint8")}


def tiles(kind, **widths):
    return {k: ("sbuf", [128, w], kind) for k, w in widths.items()}


SCRATCH = {
    **tiles("bfloat16", xt=4 * C, lvt=4 * C, ut=512, vt=512, win=8 * C, gl=4 * C, zt=4 * C, hp=4 * C, gt=12 * THIRD, yo2=4 * HALF, et=2048, one=512,
            sg=2 * C, ga=2 * C, gb=C, gp=C, pw0=2 * C, pw1=2 * C, pre=C, zero=512, town=C, tga=C, tgb=C, tpu=C, t2=C, tab2=2 * C, tl=C, tabp=2 * C,
            g1=208, g2=224, mt1=736, mt2=736, dq=88, pr=48 * len(PAIRS), qd=96 * len(QUADS)),
    **codes_of("x", C), **codes_of("u", 128), **codes_of("ur", 128), **codes_of("v", 128), **codes_of("w", 512), **codes_of("e", 512), **codes_of("z", C),
    **{"i" + n: ("sbuf", [128, w], "int32") for n, w in INTS},
    **tiles("uint16", ux=8, sel=4, ms=4, ol=32, op=32, mf=16, mo=16),
    **tiles("float32", cols=24 * len(COLS), X=128, U=96, yo=C, grt=C, gro=C),
}
for _b in range(8):
    SCRATCH["ps%d" % _b] = ("psum", [128, 512], "float32")
for _r in range(3):
    for _n in ("so", "ro", "la"):
        SCRATCH["%sR%d" % (_n, _r)] = ("sbuf", [128, 48 if _n == "so" else LW], "uint16")
        SCRATCH["%sL%d" % (_n, _r)] = ("sbuf", [128, 24], "bfloat16")
        SCRATCH["%sQ%d" % (_n, _r)] = ("sbuf", [128, 3 * THIRD + 128 if _n == "so" else 3 * THIRD], "float8_e4m3fn_x4")
        SCRATCH["%sS%d" % (_n, _r)] = ("sbuf", [128, 3 * THIRD + 128 if _n == "so" else 4 * THIRD], "uint8")
LOADS = ["lt", "rt", "x0", "x1", "u", "lv", "wc", "ws", "v"]
SEMAPHORES = (["cv", "cs", "ct", "cp", "ls", "outs"] + ["ld_" + n for n in LOADS] + ["d%d" % n for n in range(20)]
              + ["a%s%d" % (n, r) for n in "RLQS" for r in range(3)])


def route(topo, core, partner):
    ok = [c for c in topo.cores_of(core) if c != core and topo.may_write(c, partner)]
    return [c for c in ok if topo.die(c) == topo.die(core)] + [c for c in ok if topo.die(c) != topo.die(core)]


def bits(engines):
    return sum(1 << e for e in engines)


def pieces(rd, a, c, b, d):
    every = list(range(16))
    odd, even = every[1::2], every[0::2]
    out = [("R", [("R", a, 0, LW, LW, every if rd else odd)])]
    if WAYS == 5:
        out += [("L", [("L", b, 0, 24, 24, every)] if rd else [("L", b, 0, 8, 8, even[:4]), ("L", c, 8, 16, 16, odd), ("L", d, 16, 24, 24, even[4:])]),
                ("Q", [("Q", a, 0, 88, 88, odd), ("Q", b, 88, HALF, HALF, even)]), ("S", [("S", c, 0, 88, 88, odd), ("S", d, 88, HALF, HALF, even)])]
    elif WAYS == 4:
        out += [("L", [("L", b, 0, 24, 24, every)] if rd else [("L", b, 0, 8, 8, even[:4]), ("L", c, 8, 16, 16, odd), ("L", d, 16, 24, 24, even[4:])]),
                ("Q", [("Q", a, 0, THIRD, THIRD, odd[:4]), ("Q", b, THIRD, 2 * THIRD, 2 * THIRD, even[:4]), ("Q", c, 2 * THIRD, 3 * THIRD, HALF, odd[4:]),
                       ("S", d, 0, 4 * THIRD, HALF, even[4:])])]
    else:
        out += [("L", [("L", b, 0, 24, 24, every)] if rd else [("L", b, 0, 12, 12, even), ("L", c, 12, 24, 24, odd)]),
                ("Q", [("Q", a, 0, 88, 88, odd), ("Q", b, 88, HALF, HALF, even)]), ("S", [("S", c, 0, HALF, HALF, every)])]
    return out


def view(T, name, lo, hi):
    v = T[name][:, lo:hi]
    return v.bitcast(dt.uint8) if name[2] == "Q" else v


def relay_program(g, core, T, topo, rank):
    src, sent = T.cores[rank], 0
    for rd, s in enumerate(STEP):
        dst = T.cores[rank ^ s]
        for sem, parts in pieces(rd, *route(topo, src, dst)):
            for buf, relay, lo, _, hi, on in parts:
                if relay == core:
                    rid, pid = topo.addr(dst, core)
                    eng = topo.engines(core, dst)
                    g.wait_ge(T.sem["a%s%d" % (sem, rd)], len(on))
                    g.remote_dma(view(T, "la%s%d" % (buf, rd), lo, hi), view(T, "ro%s%d" % (buf, rd), lo, hi), T.sem["a%s%d" % (sem, rd)], T.sem["ls"],
                                 pid, rid, bits(eng))
                    sent += len(eng)
    if sent:
        g.wait_ge(T.sem["ls"], sent)


def rank_program(g, core, T, topo):
    rank = T.rank_of(core)
    if rank is None:
        for c in topo.cores_of(core):
            if T.rank_of(c) is not None:
                relay_program(g, core, T, topo, T.rank_of(c))
        return

    eng = {"v": g.vector, "s": g.scalar, "t": g.tensor, "p": g, "y": g.sync}
    done = {"v": "cv", "s": "cs", "t": "ct", "p": "cp"}
    count = {"cv": 0, "cs": 0, "ct": 0, "cp": 0, "outs": 0, "ls": 0}
    known = {q: {} for q in eng}
    uses = {}
    clocks = {}
    moves = []

    def meet(a, b):
        return not (a[1] >= b[2] or b[1] >= a[2] or (a[1] - b[1]) % math.gcd(a[3], b[3]))

    def before(q, reads, writes):
        need = {}
        for w, regs in ((False, reads), (True, writes)):
            for r in regs:
                ps = r[0][:2] == "ps"
                for (o, ow, oq, tok) in uses.get(r[0], []):
                    if (w or ow or (ps and oq != q)) and meet(r, o):
                        need[tok[0]] = max(need.get(tok[0], 0), tok[1])
        k = known[q]
        for s in sorted(need, key=lambda s: s in ("cv", "cs", "ct", "cp")):
            if k.get(s, 0) < need[s]:
                eng[q].wait_ge(T.sem[s], need[s])
                k[s] = need[s]
                for a, b in clocks.get((s, need[s]), {}).items():
                    k[a] = max(k.get(a, 0), b)

    def note(q, tok, reads, writes):
        clocks[tok] = dict(known[q])
        for r in writes:
            uses[r[0]] = [u for u in uses.get(r[0], []) if not (u[0][3] % r[3] == 0 and r[1] <= u[0][1] and u[0][2] <= r[2] and (u[0][1] - r[1]) % r[3] == 0)]
        for w, regs in ((False, reads), (True, writes)):
            for r in regs:
                uses.setdefault(r[0], []).append((r, w, q, tok))

    def run(q, fn, reads, writes):
        before(q, reads, writes)
        s = done[q]
        count[s] += 1
        fn().then_inc(T.sem[s], 1)
        note(q, (s, count[s]), reads, writes)

    def load(q, sem, out, in_, reg):
        before(q, [], [reg])
        eng[q].dma_start(out, in_).then_inc(T.sem[sem], 16)
        note(q, (sem, 16), [], [reg])

    def store(q, out, in_, reg):
        before(q, [reg], [])
        eng[q].dma_start(out, in_).then_inc(T.sem["outs"], 16)
        count["outs"] += 16

    def move(out, in_):
        before("y", [in_], [out])
        s = "d%d" % len(moves)
        moves.append(s)
        g.sync.dma_start(ap(out), ap(in_)).then_inc(T.sem[s], 16)
        count[s] = 16
        note("y", (s, 16), [in_], [out])

    def R(name, lo=0, hi=None, step=1):
        return (name, lo, SCRATCH[name][1][1] if hi is None else hi, step)

    def I(name, lo=0, hi=None):
        return R("i" + name, lo, hi)

    def col(name, n=1):
        return R("cols", 24 * COLS.index(name), 24 * COLS.index(name) + n)

    def P(name):
        return R("pr", 48 * PAIRS.index(name), 48 * PAIRS.index(name) + 2 * K)

    def Q(name, side=None):
        at = 96 * QUADS.index(name)
        return R("qd", at, at + 4 * K) if side is None else R("qd", at + side, at + 4 * K, 2)

    def quad(name):
        return (name, 0, C, 4)

    def pair(name, f):
        return (name, f, C, 8)

    def field(name, f):
        return (name, f, C, 16)

    def part(r, lo, hi):
        return (r[0], r[1] + lo // 16, r[1] + hi // 16, 1)

    def ap(r):
        return T[r[0]][:, r[1]:r[2]] if r[3] == 1 else T[r[0]][:, r[1]:r[2]:r[3]]

    def src(r, ind):
        return ap(r) if ind is None else ap(r).indirect(ap(ind))

    def given(*rs):
        return [r for r in rs if isinstance(r, tuple)]

    def num(s):
        return ap(s) if isinstance(s, tuple) else s

    def tt(out, in0, in1, op, ind=None):
        run("v", lambda: g.vector.tensor_tensor(ap(out), src(in0, ind), ap(in1), op), given(in0, in1, ind), [out])

    def ts(out, in0, s1, op0, s2=None, op1=None, ind=None):
        if op1 is None:
            run("v", lambda: g.vector.tensor_scalar(ap(out), src(in0, ind), num(s1), None, op0), given(in0, s1, ind), [out])
        else:
            run("v", lambda: g.vector.tensor_scalar(ap(out), src(in0, ind), num(s1), num(s2), op0, op1), given(in0, s1, s2, ind), [out])

    def cp(out, in_, ind=None):
        run("v", lambda: g.vector.tensor_copy(ap(out), src(in_, ind)), given(in_, ind), [out])

    def put(out, ind, in_):
        run("v", lambda: g.vector.tensor_copy(ap(out).indirect(ap(ind)), ap(in_)), [in_, ind], [out])

    def fill(out, c):
        run("v", lambda: g.vector.memset(ap(out), c), [], [out])

    def turn(out, in_):
        run("v", lambda: g.vector.transpose(ap(out), ap(in_)), [in_], [out])

    def act(out, in_, ind=None, func=Act.Copy, scale=1.0):
        if scale == 1.0:
            run("s", lambda: g.scalar.activation(ap(out), src(in_, ind), func), given(in_, ind), [out])
        else:
            run("s", lambda: g.scalar.activation(ap(out), src(in_, ind), func, scale=num(scale)), given(in_, ind, scale), [out])

    def shift(out, in_, scale, bias):
        run("s", lambda: g.scalar.activation(ap(out), ap(in_), Act.Identity, bias=num(bias), scale=scale), given(in_, bias), [out])

    def quant(name, tile, lo, hi, q=None, s=None, at=None):
        q, s, at = q or "q" + name, s or "s" + name, lo if at is None else at
        t = R(tile, 4 * lo, 4 * hi)
        run("v", lambda: g.vector.quantize_mx(T[q][:, at:at + hi - lo], T[s][:, at:at + hi - lo], ap(t)), [t], [R(q, at, at + hi - lo), R(s, at, at + hi - lo)])

    def mm(bank, w, wlo, q, s, lo, hi):
        p, wq, wsc = "ps%d" % bank, "q" + w, "s" + w
        run("t", lambda: g.tensor.matmul_mx(T[p][:, 0:hi - lo], T[wq][:, wlo:wlo + 128], T[wsc][:, wlo:wlo + 128], T[q][:, lo:hi], T[s][:, lo:hi], True, True),
            [R(wq, wlo, wlo + 128), R(wsc, wlo, wlo + 128), R(q, lo, hi), R(s, lo, hi)], [R(p)])

    def arrive(reg, sem, n):
        note("p", (sem, n), [], [reg])
        clocks[(sem, n)] = {}

    def iota(out, pattern, base, cm):
        run("p", lambda: g.iota(ap(out), pattern, base, cm), [], [out])

    def swap(first=None, then=None):
        turn(R("U", 0, 64), R("X", 0, 64))
        turn(R("U", 64, 96), R("X", 0, 32))
        if first:
            first()
        turn(R("X", 64, 128), R("U", 16, 80))
        if then:
            then()

    def name(k, buf, f):
        tt(R("X", 32 * k, 32 * k + K), field(buf, f), field(buf, f + 8), Op.add)

    load("y", "ld_u", T["ut"][:], T["u"][:], R("ut"))
    load("s", "ld_lt", T["ilw"][:, 0:K], T["lt"][:], I("lw"))
    load("s", "ld_rt", T["irw"][:, 0:K], T["rt"][:], I("rw"))
    for h in range(2):
        load("ys"[h], "ld_x%d" % h, T["xt"][:, 704 * h:704 * h + 704], T["x"][:, 704 * h:704 * h + 704], R("xt", 704 * h, 704 * h + 704))
    before("y", [R("xt")], [])
    load("y", "ld_lv", T["lvt"][:], T["lv"][:], R("lvt"))
    load("y", "ld_wc", T["qw"][:, 0:512].bitcast(dt.uint8), T["wc"][:, 0:2048], R("qw"))
    load("y", "ld_ws", T["sw"][:, 0:512], T["ws"][:, 0:512], R("sw"))
    load("y", "ld_v", T["vt"][:], T["v"][:], R("vt"))

    iota(I("p"), [[0, 8]], 0, 1)
    iota(I("j"), [[16, 8]], 0, 0)
    iota(I("m", 0, K), [[32, 11], [0, 2]], 0, 0)
    iota(I("o"), [[11, 2], [0, 2]], 0, 0)
    fill(R("zero"), 0.0)
    shift(R("one"), R("zero"), 0.0, 1.0)
    act(R("X"), R("zero", 0, 128))
    ts(I("c"), I("p"), 3, Op.bitwise_and)
    ts(I("d"), I("p"), 1, Op.arith_shift_right, 2, Op.bitwise_and)
    ts(I("a"), I("p"), 15, Op.bitwise_and)
    ts(I("b"), I("p"), 4, Op.arith_shift_right, 1, Op.bitwise_and)
    ts(col("mb"), I("c", 0, 1), 3.0, Op.is_equal)
    ts(col("nf"), I("c", 0, 1), 2.0, Op.is_equal, -2.0, Op.mult)
    ts(col("n2"), I("c", 0, 1), 0.0, Op.is_gt)
    tt(I("q"), I("a"), I("j"), Op.add)
    tt(col("k"), col("mb"), I("d", 0, 1), Op.add)
    cp(col("h"), I("b", 0, 1))
    ts(I("e"), I("q"), float(K), Op.is_ge)
    tt(col("sig"), col("nf"), col("n2"), Op.add)
    ts(R("ux"), I("j"), col("k"), Op.add)
    ts(I("c"), I("e"), -float(K), Op.mult)
    ts(I("d"), I("e"), 32.0, Op.mult, col("h"), Op.add)
    ts(I("b"), I("e"), -64.0, Op.mult, 32.0, Op.add)
    tt(I("q"), I("q"), I("c"), Op.add)
    ts(I("f"), I("p"), 31, Op.bitwise_and)
    ts(I("b"), I("b"), col("h"), Op.mult, 64.0, Op.add)
    ts(I("c"), I("q"), 1, Op.bitwise_and)
    ts(I("e"), I("q"), 62, Op.bitwise_and)
    ts(col("f1"), I("a", 0, 1), float(ID), Op.is_equal, float(C), Op.mult)
    ts(I("c"), I("c"), col("h"), Op.not_equal)
    tt(I("q"), I("e"), I("d"), Op.add)
    cp(col("p32"), I("f", 0, 1))
    tt(I("c"), I("c"), I("b"), Op.mult)
    act(R("pw0", 0, C), R("zero", 0, C))
    act(R("ga", C, 2 * C), R("zero", 0, C))
    act(R("t2"), R("zero", 0, C))
    quant("u", "ut", 0, 128)
    tt(I("q"), I("q"), I("c"), Op.add)
    run("v", lambda: g.vector.tensor_copy(T["qur"][:].bitcast(dt.uint32), T["qu"][:].bitcast(dt.uint32).indirect(T["ux"][:])), [R("qu"), R("ux")], [R("qur")])
    run("s", lambda: g.scalar.activation(T["sur"][:], T["su"][:].indirect(T["ux"][:]), Act.Copy), [R("su"), R("ux")], [R("sur")])
    cp(R("sel"), I("q", 0, 4))
    for b in range(4):
        run("p", lambda: g.affine_select(T["et"][:, 512 * b:512 * b + 512], T["one"][:], [[-1, 512]], Op.is_equal, 0.0, b, 4),
            [R("one")], [R("et", 512 * b, 512 * b + 512)])

    def scores(bank, lo, hi):
        for k in range(2):
            mm(bank + k, "ur", 0, "qx", "sx", lo, hi)
        act(R("sg", C + lo, C + hi), R("ps%d" % (bank + 1), 0, hi - lo), func=Act.Sign, scale=col("mb"))

    def flags(bank, lo, hi):
        ts(R("sg", lo, hi), R("ps%d" % bank, 0, hi - lo), col("sig"), Op.mult, 0.0, Op.is_gt)

    cp(R("X", 0, K), I("rw", 0, K))
    cp(R("X", 32, 32 + K), I("lw", 0, K))
    quant("x", "xt", 0, HALF)
    scores(0, 0, HALF)
    swap(lambda: cp(R("ol", 0, K), I("lw", 0, K)), lambda: flags(0, 0, HALF))
    cp(I("n"), R("X"), R("sel", 0, 3))
    quant("x", "xt", HALF, C)
    scores(2, HALF, C)
    ts(I("lo"), I("n"), 31, Op.bitwise_and)
    tt(I("o"), I("o"), I("a", 0, 4), Op.add)
    for f, at in ((0, K), (1, 0)):
        tt(R("dq", f, 88, 4), I("n", at, at + K), I("lo", at, at + K), Op.subtract)
        cp(R("dq", f + 2, 88, 4), I("lo", at, at + K))
    flags(2, HALF, C)
    ts(I("c", 0, 4), I("o"), col("h"), Op.add)
    turn(R("town"), R("sg", 0, C))
    cp(field("t2", ID), I("m", 0, K))
    cp(quad("town"), R("dq"))
    ts(field("t2", ID + 8), R("zero", 0, K), col("p32"), Op.add)
    turn(R("sg", 0, C), R("town"))

    def plane(t):
        act(R("win", 704 * t, 704 * t + C), R("xt", t, 4 * C, 4), scale=0.5)

    def differences(own):
        l, r = pair(own, L), pair(own, RT)
        return [lambda: tt(Q("D"), quad("tga"), quad(own), Op.subtract), lambda: tt(P("E"), l, pair("tga", RT), Op.subtract),
                lambda: tt(P("Z"), pair("tpu", RT), r, Op.subtract), lambda: tt(P("El"), r, l, Op.subtract)]

    def step(j, own, out, ol, ready, pw, gap):
        pos, neg, way = 1 + 4 * j, 2 + 4 * j, 3 + 4 * j
        act(R("ga", 0, C), R("sg"), ol, func=Act.Relu)
        act(R("gb"), R("ga"), ol)
        gap()
        d = differences(own)
        if ready:
            cp(R("gp"), R("sg"), R("op", 0, K))
            turn(R("tga"), R("ga", 0, C))
            turn(R("tpu"), R("gp"))
        else:
            put(R(pw), ol, R("sg", 0, C))
            turn(R("tga"), R("ga", 0, C))
            turn(R("tpu"), R(pw, 0, C))
            turn(R("tgb"), R("gb"))
            d[0]()
        tt(P("act"), pair("town", pos), pair("tga", neg), Op.mult)
        tt(P("acd"), pair("town", neg), pair("tpu", pos), Op.mult)
        late = lambda: tt(P("at"), P("act"), pair("tgb", way), Op.mult)
        if not ready:
            d[2](), d[1]()
            late()
        tt(Q("M", 1), P("act"), Q("D", 1), Op.mult)
        tt(P("dt"), P("acd"), pair("tga", way), Op.mult)
        tt(P("m4"), P("acd"), P("Z"), Op.mult)
        if ready:
            tt(Q("M", 0), P("dt"), P("El"), Op.mult)
            turn(R("tgb"), R("gb"))
            tt(Q("A"), quad(own), Q("M"), Op.add)
            late()
            a, at = Q("A"), P("at")
            tt(col("n2", K), (a[0], a[1], a[2], 4), (a[0], a[1] + 2, a[2], 4), Op.add)
            tt(col("nf", K), (at[0], at[1], at[2], 2), col("dn", K), Op.mult)
            tt(Q("N", 0), at, Q("D", 0), Op.mult)
            tt(R("X", 0, K), col("n2", K), col("nf", K), Op.add)
            tt(Q("N", 1), at, P("E"), Op.mult)
            tt(Q("A", 1), Q("A", 1), P("m4"), Op.add)
            swap(lambda: tt(quad(out), a, Q("N"), Op.add), lambda: turn(R("sg", 0, C), R(out)))
            return
        tt(Q("N", 0), P("at"), Q("D", 0), Op.mult)
        if not ready:
            tt(Q("M", 0), P("dt"), P("El"), Op.mult)
        tt(Q("N", 1), P("at"), P("E"), Op.mult)
        if not ready:
            tt(Q("A"), quad(own), Q("M"), Op.add)
            tt(Q("N", 1), Q("N", 1), P("m4"), Op.add)
        tt(quad(out), Q("A"), Q("N"), Op.add)

    differences("town")[3]()
    ll = R("ol", 0, K)
    for rd in range(3):
        last = rd == 2
        partner = T.cores[rank ^ STEP[rd]]
        plan = pieces(rd, *route(topo, core, partner))
        q, s, lists = "soQ%d" % rd, "soS%d" % rd, "soR%d" % rd

        def remote(k):
            sem, parts = plan[k]
            before("p", [R("so%s%d" % (buf, rd), lo, hi) for buf, _, lo, hi, _, _ in parts], [])
            tr, total = [], sum(len(topo.engines(p[1], partner)) for p in parts)
            for buf, relay, lo, hi, end, on in parts:
                rid, pid = topo.addr(relay, core)
                tr.append(RemoteDMATransfer(dst_ids=[DstId(rid=rid, pnc=pid)], dma_engine_mask=bits(topo.engines(core, relay)[e] for e in on),
                                            remote_sem=T.sem["a%s%d" % (sem, rd)],
                                            src=view(T, "so%s%d" % (buf, rd), lo, hi), dst=view(T, "ro%s%d" % (buf, rd), lo, hi)))
                arrive(R("la%s%d" % (buf, rd), lo, end), "a%s%d" % (sem, rd), total)
            g.remote_dma_fused(tr, local_sem=T.sem["ls"])
            count["ls"] += sum(len(p[5]) for p in parts)

        def gap0():
            if rd == 0:
                act(R("pw1", 0, C), R("zero", 0, C))
            for t in range(4):
                plane(t)

        def gap1():
            for t in range(4):
                if rd == 0:
                    act(R("win", 704 * t + C, 704 * t + 2 * C), R("lvt", t, 4 * C, 4), scale=0.5)
                else:
                    act(R("win", 704 * t + C, 704 * t + C + HALF), R("ps%d" % (4 + t), 0, HALF), scale=0.5)
                    act(R("win", 704 * t + C + HALF, 704 * t + 2 * C), R("yo2", HALF * t, HALF * t + HALF), scale=0.5)
            if rd == 0:
                shift(R("pre"), R("zero", 0, C), 0.0, col("f1"))
                for o in (R("g1"), R("gt", 4 * HALF, 12 * THIRD), R("mt1", 192, C), R("mt1", 544, 736), R("tl"), R("g2", 192, 224), R("mt2", C, 544)):
                    move(o, R("zero", 0, o[2] - o[1]))

        step(0, "town" if rd == 0 else "t2", "town", ll, rd > 0, "pw0", gap0)
        if rd == 0:
            ts(I("c", 0, 4), I("c", 0, 4), 1, Op.bitwise_and)
            name(0, "town", L)
            ts(I("o"), I("o"), 16.0, Op.mult, float(COL), Op.add)
            swap(lambda: turn(R("sg", 0, C), R("town")), lambda: ts(I("c", 0, 4), I("c", 0, 4), C + 16.0, Op.mult))
        cp(R("ol"), R("X"), R("sel", 0, 2))
        differences("town")[3]()
        step(1, "town", "t2", R("ol", 0, K), False, "pw1", gap1)
        fill(R("soL%d" % rd, K, 24), 0.0)
        name(0, "t2", RT)
        name(1, "t2", L)
        nl = R("X", 32, 32 + K)
        swap(lambda: ts(col("nf", K), nl, float(C), Op.is_ge, -float(C), Op.mult), lambda: ts(col("n2", K), nl, -float(HALF), Op.add))
        cp(R(lists), R("X"), R("sel", 0, 3))
        remote(0)
        tt(field("t2", COL), col("n2", K), col("nf", K), Op.add)
        tt(R("soL%d" % rd, 0, K), col("n2", K), col("nf", K), Op.add)
        remote(1)
        turn(R("tab2", 0, C), R("t2"))
        move(R("tab2", C, 2 * C), R("tab2", 0, C))
        if WAYS == 4:
            quant("", "zero", 0, 128, q, s, 3 * THIRD)
        if not last:
            move(R("pw1", 0, C), R("zero", 0, C))
        if rd == 0:
            move(R("pw0", 0, C), R("pre"))
            tt(I("c", 0, 4), I("c", 0, 4), I("o"), Op.add)
        lr, ll = R(lists, 0, K), R(lists, K, 2 * K)

        def layer(h, b, on):
            lo, hi = CHUNKS[h]
            o, i = R("hp", C * b + lo, C * b + hi), R("ps%d" % (4 * h + b), 0, hi - lo)
            if on == "v":
                ts(o, i, 0.03125, Op.mult)
            else:
                act(o, i, scale=0.03125)

        for h, (lo, hi) in enumerate(CHUNKS):
            for t in range(4):
                act(R("gl", C * t + lo, C * t + hi), R("win", 704 * t, 704 * t + 704), part(ll, lo, hi))
            for t in range(4 * h):
                layer(0, t, "s")
            for t in range(4):
                tt(R("zt", 4 * lo + t, 4 * hi, 4), R("win", 704 * t, 704 * t + 704), R("gl", C * t + lo, C * t + hi), Op.add, part(lr, lo, hi))
            quant("z", "zt", lo, hi)
            for b in range(4):
                mm(4 * h + b, "w", 128 * b, "qz", "sz", lo, hi)
        act(R("g1", 16, 192), R("tab2"), R("laR%d" % rd, 0, 11))
        push = [lambda lo=lo, hi=hi: put(R("pw0"), part(ll, lo, hi), R("tab2", lo, hi)) for lo, hi in CHUNKS]
        wanted = [lambda: turn(R("mt1", 0, 192), R("g1", 16, 208)), lambda: turn(R("mt1", C, C + 192), R("g1", 0, 192)),
                  lambda: ts(R("mf"), R("mt1"), float(HALF), Op.add, ind=R("ms", 0, 1))]
        if rd == 0:
            ts(R("ms"), I("c", 0, 4), 735.0, Op.min)
            quant("e", "et", 0, 512)
            for b in range(4):
                layer(1, b, "v")
            push[0]()
            wanted[0](), wanted[1](), wanted[2]()
        else:
            wanted[0](), wanted[1]()
            layer(1, 0, "v"), layer(1, 1, "s")
            wanted[2]()
            layer(1, 2, "v"), layer(1, 3, "s")
        for b in range(4):
            (act if b % 2 else cp)(R("gt", b, 4 * HALF, 4), R("hp", C * b, C * b + C), R("mf", 0, 11))
        quant("", "gt", 0, 3 * THIRD if WAYS == 4 else HALF, q, s)
        for k in range(2, len(plan)):
            remote(k)
        if not last:
            act(R("ga", 0, C), R("tab2"), ll)
        cp(field("tl", COL), R("laL%d" % rd, 0, K))
        turn(R("tabp", 0, C), R("tl"))
        turn(R("tabp", C, 2 * C), R("tl"))
        act(R("g2", 0, 192), R("tabp"), part(lr, 160, C))
        if rd == 1:
            push[0]()
        if last:
            fill(R("grt"), 0.0)
            quant("v", "vt", 0, 128)
            cp(field("grt", 0), R("X", 32, 32 + K))
            cp(field("grt", 1), R("X", 0, K))
        turn(R("mt2", 160, C), R("g2", 0, 192))
        turn(R("mt2", C + 192, 736), R("g2", 16, 208))
        if not last:
            turn(R("tga"), R("ga", 0, C))
        ts(R("mo"), R("mt2"), float(HALF), Op.add, ind=R("ms", 2, 3))
        own = R("mo", 0, 11)
        for b in range(4):
            if not last or b % 2:
                act(R("yo2", HALF * b, HALF * b + HALF), R("hp", C * b, C * b + C), own)

        def owns(b):
            x = R("xt", 4 * HALF + b, 4 * C, 4)
            if not last or b % 2:
                tt(x, R("yo2", HALF * b, HALF * b + HALF), x, Op.add)
            else:
                tt(x, R("hp", C * b, C * b + C), x, Op.add, own)
        if not last:
            push[1]()
            owns(0)
            turn(R("tpu"), R("pw0", 0, C))
            owns(1)
            name(0, "tpu", ID)
            owns(2)
            if rd == 0:
                move(R("pw0", 0, C), R("pre"))
            swap(lambda: owns(3))
            quant("x", "xt", HALF, C)
            scores(0, HALF, C)
            cp(R("op"), R("X"), R("sel", 0, 2))
            flags(0, HALF, C)
        else:
            owns(0), owns(2), owns(1), owns(3)
            quant("x", "xt", HALF, C)
            mm(0, "v", 0, "qx", "sx", HALF, C)
            turn(R("gro"), R("grt"))
            act(R("yo", HALF, C), R("ps0", 0, HALF))
            store("y", T["oc"][:, 4 * HALF:4 * C], T["qx"][:, HALF:C].bitcast(dt.uint8), R("qx", HALF, C))
            for k in range(4):
                store("y", T["osc"][4 * k:4 * k + 4, HALF:C], T["sx"][32 * k:32 * k + 4, HALF:C], R("sx", HALF, C))
            for k in range(2):
                store("y", T["gr"][:, C * k:C * k + C], T["gro"][k:128:16, :], R("gro"))
            store("y", T["y"][:, HALF:C], T["yo"][:, HALF:C], R("yo", HALF, C))
        for b in range(4):
            mm(4 + b, "e", 128 * b, "laQ%d" % rd, "laS%d" % rd, 0, HALF)
        for b in range(4):
            x = R("xt", b, 4 * HALF, 4)
            tt(x, R("ps%d" % (4 + b), 0, HALF), x, Op.add)
        quant("x", "xt", 0, HALF)
        if not last:
            scores(2, 0, HALF)
            for f in differences("t2"):
                f()
            d = Q("D")
            tt(col("dn", K), (d[0], d[1], d[2], 4), (d[0], d[1] + 2, d[2], 4), Op.add)
            flags(2, 0, HALF)
            turn(R("town"), R("sg", 0, C))
    mm(1, "v", 0, "qx", "sx", 0, HALF)
    store("y", T["oc"][:, 0:4 * HALF], T["qx"][:, 0:HALF].bitcast(dt.uint8), R("qx", 0, HALF))
    for k in range(4):
        store("s" if k == 0 else "y", T["osc"][4 * k:4 * k + 4, 0:HALF], T["sx"][32 * k:32 * k + 4, 0:HALF], R("sx", 0, HALF))
    cp(R("yo", 0, HALF), R("ps1", 0, HALF))
    store("s", T["y"][:, 0:HALF], T["yo"][:, 0:HALF], R("yo", 0, HALF))
    for s in sorted(count):
        g.wait_ge(T.sem[s], count[s])
